import numpy as np
import ml_dtypes


def mxq(x, axis, fmt="e4m3"):
    dtype, down = {"e4m3": (ml_dtypes.float8_e4m3fn, 7), "e5m2": (ml_dtypes.float8_e5m2, 14)}[fmt]
    v = np.moveaxis(np.asarray(x, np.float32).astype(ml_dtypes.bfloat16).astype(np.float64), axis, -1)
    blocks = v.reshape(v.shape[:-1] + (-1, 32))
    amax = np.abs(blocks).max(-1, keepdims=True)
    byte = np.maximum(np.where(amax > 0, np.frexp(amax)[1] - 1 + 127, 0) - down, 1)
    scale = np.exp2(byte - 127.0)
    codes = (blocks / scale).astype(np.float32).astype(dtype).astype(np.float64)
    return np.moveaxis((codes * scale).reshape(v.shape), -1, axis)


WIDE = False


def mx_kscale(k):
    if not WIDE:
        return np.ones(k)
    levels = np.array([10, -10, 5, -5, 0])
    if k % 512:
        return np.exp2(np.random.permutation(np.resize(levels, k // 32))).repeat(32)
    a = np.empty((k // 512, 16))
    for p in range(k // 512):
        a[p, :8] = np.random.permutation(np.resize(levels, 8))
        for g in range(8):
            far = levels[np.abs(levels - a[p, g]) >= 10]
            a[p, g + 8] = far[np.random.randint(len(far))]
    return np.exp2(a.ravel()).repeat(32)


def f64(x):
    return np.asarray(x).astype(np.float64)


def striped(idx):
    return np.tile(idx.reshape(-1, 16).T, (8, 1)).astype(np.uint16)


def unstriped(offs):
    return offs[:16].T.reshape(-1).astype(np.int64)


E2M1 = np.array([0.0, 0.5, 1.0, 1.5, 2.0, 3.0, 4.0, 6.0, -0.0, -0.5, -1.0, -1.5, -2.0, -3.0, -4.0, -6.0])


def pack_weight(w, fmt):
    k, n = w.shape
    w = f64(np.asarray(w, np.float32).astype(ml_dtypes.bfloat16)).reshape(k // 32, 32, n)
    amax = np.abs(w).max(1)
    if fmt == "e4m3":
        byte = np.frexp(amax)[1] - 1 + 127 - 7
    else:
        mant, ex = np.frexp(amax / 6.0)
        byte = np.where(mant > 0.5, ex, ex - 1) + 127
    byte = np.clip(np.where(amax > 0, byte, 1), 1, 254)
    scaled = (w * np.exp2(127.0 - byte)[:, None, :]).reshape(k, n).astype(np.float32)
    by_word = np.ascontiguousarray(scaled.reshape(k // 512, 128, 4, n).transpose(0, 1, 3, 2))
    if fmt == "e4m3":
        words = by_word.astype(ml_dtypes.float8_e4m3fn).view(np.uint8)
    else:
        c = by_word.astype(ml_dtypes.float4_e2m1fn).view(np.uint8) & 0xF
        words = (c[..., 0::2] | (c[..., 1::2] << 4)).reshape(k // 512, 128, 2 * n)
    return np.ascontiguousarray(words), np.ascontiguousarray(byte.astype(np.uint8).reshape(k // 512, 16, n))


def unpack_weight(words, scales, fmt):
    g, _, n = scales.shape
    words = np.ascontiguousarray(words).reshape(g, 128, n, -1)
    if fmt == "e4m3":
        vals = words.view(ml_dtypes.float8_e4m3fn).astype(np.float64)
    else:
        nib = np.empty((g, 128, n, 4), np.uint8)
        nib[..., 0::2] = words & 0xF
        nib[..., 1::2] = words >> 4
        vals = E2M1[nib]
    vals = vals * np.repeat(np.exp2(scales.astype(np.float64) - 127.0), 8, axis=1)[..., None]
    return vals.transpose(0, 1, 3, 2).reshape(g * 512, n)


def gelu(v):
    return 0.5 * v * (1.0 + np.tanh(np.sqrt(2.0 / np.pi) * (v + 0.044715 * v**3)))


def striped8(idx):
    return np.concatenate([v.reshape(-1, 16).T for v in idx]).astype(np.uint16)


def unstriped8(offs):
    return np.stack([offs[16 * g:16 * g + 16].T.reshape(-1) for g in range(8)]).astype(np.int64)


def put_heads(h, wgs, idx8, t2):
    r = np.arange(h.shape[0])
    page = np.zeros((h.shape[0], t2))
    page[r[:, None], idx8[r % 512 // 64]] = wgs[r // 4 % 128] * h
    return page


K, T, S, H, T2, P, N = 512, 4096, 1024, 1024, 2048, 1024, 384

def setup_inputs():
    n = np.random.standard_normal
    s = mx_kscale(K)[:, None]
    u = mx_kscale(H)[:, None]
    tab_words, tab_scales = pack_weight(n((K, T)) * s, "e4m3")
    w1_words, w1_scales = pack_weight(1.6 * n((K, H)) / np.sqrt(K) / s, "e2m1")
    w2 = 1.2 * n((K, H)) / np.sqrt(K) / s * u.T
    w3 = n((H, N)) / np.sqrt(H) / u
    w4_words, w4_scales = pack_weight(n((H, N)) / np.sqrt(H) / u, "e4m3")
    slots = np.stack([np.random.permutation(T2)[:S] for _ in range(8)])
    return {
        "tab_words": tab_words, "tab_scales": tab_scales,
        "offs": striped(np.random.permutation(T)[:S]),
        "w1_words": w1_words, "w1_scales": w1_scales,
        "w2": w2.astype(np.float32),
        "offs2": striped8(slots),
        "wgs": np.repeat(np.random.uniform(0.5, 2.0, (8, S)), 16, axis=0).astype(np.float32),
        "offs3": striped(np.random.permutation(T2)[:P]),
        "flow": (0.7 * n((H, P)) * u).astype(np.float32),
        "liner": (0.5 * n(H) * u[:, 0]).astype(np.float32),
        "w3": w3.astype(np.float32),
        "bias": (0.6 * n(N)).astype(np.float32),
        "w4_words": w4_words, "w4_scales": w4_scales,
    }

def reference(tab_words, tab_scales, offs, w1_words, w1_scales, w2, offs2, wgs, offs3, flow, liner, w3, bias, w4_words, w4_scales):
    v = unpack_weight(tab_words, tab_scales, "e4m3")[:, unstriped(offs)]
    w1 = unpack_weight(w1_words, w1_scales, "e2m1")
    w4 = unpack_weight(w4_words, w4_scales, "e4m3")
    phase = np.tanh(w1.T @ v)
    level = np.abs(mxq(f64(w2), 0, "e4m3").T @ v)
    h = phase * level
    page = put_heads(h, f64(wgs), unstriped8(offs2), T2)
    x = page[:, unstriped(offs3)]
    z = mxq(x + f64(flow) + f64(liner)[:, None], 0, "e4m3")
    y1 = (mxq(f64(w3), 0, "e4m3").T @ z) + f64(bias)[:, None]
    y2 = w4.T @ z
    return np.maximum(y1, y2)

@@ -1,0 +1,273 @@
+from contextlib import ExitStack
+
+import concourse.mybir as mybir
+
+K, T, S, H, T2, M, N = 512, 4096, 1024, 1024, 2048, 1024, 384
+FLOPS = 2 * (2 * K * H * S + 2 * H * N * M)
+
+F32 = mybir.dt.float32
+BF16 = mybir.dt.bfloat16
+I32 = mybir.dt.int32
+U32 = mybir.dt.uint32
+U16 = mybir.dt.uint16
+U8 = mybir.dt.uint8
+FP8X4 = mybir.dt.float8_e4m3fn_x4
+FP4X4 = mybir.dt.float4_e2m1fn_x4
+ACT = mybir.ActivationFunctionType
+ALU = mybir.AluOpType
+
+P = 128
+PACK = 4
+K_PASS = P * PACK
+BANK = 512
+PASSES = H // K_PASS
+N_TILES = N // P
+LAST_CHUNKS = (256, 256, 256, 128, 128)
+
+
+def tile_list_duct_mode_features_kernel(
+    tc, tab_words, tab_scales, offs, w1_words, w1_scales, w2, offs2, wgs, offs3, flow, liner, w3, bias,
+    w4_words, w4_scales, out,
+):
+    nc = tc.nc
+
+    with ExitStack() as ctx:
+        keep = ctx.enter_context(tc.tile_pool(name="keep", bufs=1))
+        ring = ctx.enter_context(tc.tile_pool(name="ring", bufs=2))
+
+        def load_scale_rows(queue, plane, rows):
+            by_r = rows.rearrange("a (q r) c -> r q a c", r=4)
+            for r in range(4):
+                queue.dma_start(out=plane[r:P:32, :, :].bitcast(I32), in_=by_r[r].bitcast(I32))
+
+        idx1 = keep.tile([P, S // 16], U16, name="idx1")
+        idx2 = keep.tile([P, S // 16], U16, name="idx2")
+        idx3 = keep.tile([P, M // 16], U16, name="idx3")
+        nc.sync.dma_start(idx1[:], offs)
+        w1_raw = keep.tile([P, 2 * H], U8, name="w1_raw", tag="w1_then_wgs")
+        nc.sync.dma_start(out=w1_raw[:].bitcast(I32), in_=w1_words[0].bitcast(I32))
+        nc.sync.dma_start(idx2[:], offs2)
+        nc.sync.dma_start(idx3[:], offs3)
+
+        w2_by_pass = w2.rearrange("(p j) (b c) -> b p j c", j=PACK, b=PASSES)
+
+        def load_w2(b):
+            raw = keep.tile([P, PACK, K_PASS], F32, name="w2_raw%d" % b, tag="weights_raw")
+            nc.sync.dma_start(out=raw[:], in_=w2_by_pass[b])
+            return raw
+
+        w2_raw = load_w2(0)
+        table = keep.tile([P, T], U32, name="table")
+        nc.sync.dma_start(out=table[:].bitcast(I32), in_=tab_words[0].rearrange("p t i -> p (t i)").bitcast(I32))
+
+        table_s = keep.tile([P, T], U8, name="table_s")
+        nc.vector.memset(table_s[:].bitcast(I32), 0)
+        load_scale_rows(nc.scalar, table_s[:].rearrange("p (a c) -> p a c", a=1), tab_scales)
+
+        w1s_raw = keep.tile([P, H], U8, name="w1s_raw", tag="w1s_then_flow0", align_bytes=64)
+        nc.gpsimd.memset(w1s_raw[:].bitcast(I32), 0)
+        load_scale_rows(nc.gpsimd, w1s_raw[:].rearrange("p (a c) -> p a c", a=1), w1_scales)
+
+        pages = [keep.tile([P, T2], F32, name="page%d" % t) for t in range(PACK)]
+        for t in range(PACK):
+            (nc.vector if t < 2 else nc.gpsimd).memset(pages[t][:], 0.0)
+
+        liner_sb = keep.tile([P, PASSES, PACK], F32, name="liner_sb")
+        nc.gpsimd.dma_start(out=liner_sb[:], in_=liner.rearrange("(b p t) -> p b t", b=PASSES, t=PACK))
+        bias_sb = keep.tile([P, N_TILES], F32, name="bias_sb")
+        with nc.allow_non_contiguous_dma(reason="one bias value for each partition and output tile"):
+            nc.gpsimd.dma_start(out=bias_sb[:], in_=bias.rearrange("(n p) -> p n", p=P))
+        w4_s = keep.tile([P, PASSES, N], U8, name="w4_s", align_bytes=64)
+        nc.gpsimd.memset(w4_s[:].rearrange("p a c -> p (a c)").bitcast(I32), 0)
+        load_scale_rows(nc.gpsimd, w4_s[:], w4_scales)
+
+        w1_c = keep.tile([P, 2 * H], U8, name="w1_c", align_bytes=64)
+        nc.vector.tensor_copy(
+            out=w1_c[:].rearrange("p (b t q e) -> p b t q e", b=PASSES, t=PACK, e=2),
+            in_=w1_raw[:].rearrange("p (b q t e) -> p b t q e", b=PASSES, t=PACK, e=2),
+        )
+        w1_s = keep.tile([P, H], U8, name="w1_s", align_bytes=64)
+        nc.vector.tensor_copy(
+            out=w1_s[:].rearrange("p (b t q) -> p b t q", b=PASSES, t=PACK),
+            in_=w1s_raw[:].rearrange("p (b q t) -> p b t q", b=PASSES, t=PACK),
+        )
+        wgs_sb = keep.tile([P, S], F32, name="wgs_sb", tag="w1_then_wgs")
+        nc.sync.dma_start(out=wgs_sb[:], in_=wgs)
+
+        flow_by_pass = flow.rearrange("(b p t) m -> b p t m", b=PASSES, t=PACK)
+
+        def load_flow(b, tag):
+            rows = keep.tile([P, PACK, M], F32, name="flow%d" % b, tag=tag, align_bytes=64)
+            nc.sync.dma_start(out=rows[:], in_=flow_by_pass[b])
+            return rows
+
+        def add_liner(rows, b):
+            for t in range(PACK):
+                nc.scalar.activation(rows[:, t, :], rows[:, t, :], ACT.Identity, bias=liner_sb[:, b, t : t + 1])
+
+        def quantize(width, rounded, name):
+            codes = keep.tile([P, width], U32, name=name + "_c", align_bytes=64)
+            scales = keep.tile([P, width], U8, name=name + "_s", align_bytes=64)
+            nc.vector.quantize_mx(out=codes[:].bitcast(FP8X4), scales=scales[:], in_=rounded)
+            return codes, scales
+
+        def quantize_w2(raw, b, tag):
+            rounded = keep.tile([P, PACK * K_PASS], BF16, name="w2_bf%d" % b, tag=tag, align_bytes=64)
+            nc.scalar.copy(
+                out=rounded[:].rearrange("p (t q j) -> p q j t", t=PACK, j=PACK),
+                in_=raw[:].rearrange("p j (q t) -> p q j t", t=PACK),
+            )
+            return quantize(K_PASS, rounded[:], "w2q%d" % b)
+
+        def round_and_quantize(planes, width, name):
+            rounded = ring.tile([P, PACK * width], BF16, name="rounded", tag="rounded", align_bytes=64)
+            nc.scalar.copy(
+                out=rounded[:].rearrange("p (c i t) -> p c t i", i=4, t=PACK),
+                in_=planes.rearrange("p t (c i) -> p c t i", i=4),
+            )
+            return quantize(width, rounded[:], name)
+
+        w2_q = [quantize_w2(w2_raw, 0, "w2bf_then_flow1")]
+
+        v_s = keep.tile([P, S], U8, name="v_s", align_bytes=64)
+        nc.vector.tensor_copy(v_s[:], table_s[:].indirect(idx1[:]))
+        v_c = []
+        for half in range(S // BANK):
+            words = keep.tile([P, BANK], U32, name="v_c%d" % half, align_bytes=64)
+            nc.vector.tensor_copy(words[:], table[:].indirect(idx1[:, half * 32 : (half + 1) * 32]))
+            v_c.append(words)
+
+        flows = [load_flow(0, "w1s_then_flow0")]
+        w2_raw = load_w2(1)
+        w4_c = keep.tile([P, PASSES, N], U32, name="w4_c", align_bytes=64)
+        z0 = keep.tile([P, PACK, M], F32, name="z0")
+        z0_q = []
+        w3_q = []
+
+        with tc.psum_pool(name="stage1", bufs=2) as psum1:
+
+            def features(s):
+                b, t = divmod(s, PACK)
+                phase = ring.tile([P, S], F32, name="phase", tag="phase", bufs=3)
+                level = ring.tile([P, S], F32, name="level", tag="level")
+                for half in range(S // BANK):
+                    cols = slice(half * BANK, (half + 1) * BANK)
+                    acc1 = psum1.tile([P, BANK], F32, name="acc1", tag="acc1")
+                    nc.tensor.matmul_mx(
+                        out=acc1[:],
+                        lhsT=w1_c[:, s * 2 * P : (s + 1) * 2 * P].bitcast(FP4X4),
+                        lhsT_scale=w1_s[:, s * P : (s + 1) * P],
+                        rhs=v_c[half][:].bitcast(FP8X4),
+                        rhs_scale=v_s[:, cols],
+                        start=True,
+                        stop=True,
+                    )
+                    nc.scalar.activation(phase[:, cols], acc1[:], ACT.Tanh)
+                    acc2 = psum1.tile([P, BANK], F32, name="acc2", tag="acc2")
+                    nc.tensor.matmul_mx(
+                        out=acc2[:],
+                        lhsT=w2_q[b][0][:, t * P : (t + 1) * P].bitcast(FP8X4),
+                        lhsT_scale=w2_q[b][1][:, t * P : (t + 1) * P],
+                        rhs=v_c[half][:].bitcast(FP8X4),
+                        rhs_scale=v_s[:, cols],
+                        start=True,
+                        stop=True,
+                    )
+                    nc.scalar.activation(level[:, cols], acc2[:], ACT.Abs)
+                return phase, level
+
+            def product(pair, lo, hi):
+                phase, level = pair
+                nc.vector.tensor_tensor(phase[:, lo:hi], phase[:, lo:hi], level[:, lo:hi], ALU.mult)
+
+            def put(pair, s, lo, hi):
+                nc.vector.tensor_tensor(
+                    pages[s % PACK][:].indirect(idx2[:, lo // 16 : hi // 16]), pair[0][:, lo:hi], wgs_sb[:, lo:hi],
+                    ALU.mult,
+                )
+
+            def fetch(dst, b, t, lo, hi):
+                nc.vector.tensor_tensor(
+                    dst, pages[t][:].indirect(idx3[:, lo // 16 : hi // 16]), flows[b][:, t, lo:hi], ALU.add
+                )
+
+            pair = features(0)
+            for lo in range(0, S, BANK):
+                product(pair, lo, lo + BANK)
+            for s in range(PASSES * PACK):
+                nxt = None
+                if s == 0:
+                    for lo in range(0, S, BANK):
+                        put(pair, s, lo, lo + BANK)
+                    add_liner(flows[0], 0)
+                if s == 2:
+                    w2_q.append(quantize_w2(w2_raw, 1, "w2bf1"))
+                    flows.append(load_flow(1, "w2bf_then_flow1"))
+                    w3_raw = keep.tile([P, PASSES, PACK, N], F32, name="w3_raw", tag="weights_raw")
+                    nc.sync.dma_start(
+                        out=w3_raw[:].rearrange("p a j n -> p a (j n)"),
+                        in_=w3.rearrange("(a p j) n -> p a (j n)", a=PASSES, j=PACK),
+                    )
+                    nc.sync.dma_start(
+                        out=w4_c[:].bitcast(I32),
+                        in_=w4_words.rearrange("a p n i -> p a (n i)").bitcast(I32),
+                    )
+                if s + 1 < PASSES * PACK:
+                    nxt = features(s + 1)
+                    product(nxt, 0, S)
+                if s > 0:
+                    put(pair, s, 0, S)
+                if 1 <= s <= PACK:
+                    fetch(z0[:, s - 1, :], 0, s - 1, 0, M)
+                if s == PACK:
+                    for lo in range(0, M, BANK):
+                        z0_q.append(round_and_quantize(z0[:, :, lo : lo + BANK], BANK, "z0q%d" % lo))
+                if s == PACK + 1:
+                    add_liner(flows[1], 1)
+                    for a in range(PASSES):
+                        w3_q.append(round_and_quantize(w3_raw[:, a], N, "w3q%d" % a))
+                pair = nxt
+
+        out_by_tile = out.rearrange("(n p) m -> p n m", p=P)
+        with tc.psum_pool(name="stage2", bufs=8) as psum2:
+            lo = 0
+            for width in LAST_CHUNKS:
+                hi = lo + width
+                z1 = ring.tile([P, PACK, width], F32, name="z1", tag="z1", bufs=3)
+                for t in range(PACK):
+                    fetch(z1[:, t, :], 1, t, lo, hi)
+                z1_q = round_and_quantize(z1[:], width, "z1q%d" % lo)
+                zc0, zs0 = z0_q[lo // BANK]
+                z0_cols = slice(lo % BANK, lo % BANK + width)
+                moving = ((zc0[:, z0_cols], zs0[:, z0_cols]), (z1_q[0][:], z1_q[1][:]))
+                result = ring.tile([P, N_TILES, width], F32, name="result", tag="result", bufs=3)
+                for n in range(N_TILES):
+                    rows = slice(n * P, (n + 1) * P)
+                    acc = psum2.tile([P, 2 * width], F32, name="acc", tag="acc")
+                    for a in range(PASSES):
+                        codes, scales = moving[a]
+                        nc.tensor.matmul_mx(
+                            out=acc[:, :width],
+                            lhsT=w3_q[a][0][:, rows].bitcast(FP8X4),
+                            lhsT_scale=w3_q[a][1][:, rows],
+                            rhs=codes.bitcast(FP8X4),
+                            rhs_scale=scales,
+                            start=(a == 0),
+                            stop=False,
+                        )
+                        nc.tensor.matmul_mx(
+                            out=acc[:, width:],
+                            lhsT=w4_c[:, a, rows].bitcast(FP8X4),
+                            lhsT_scale=w4_s[:, a, rows],
+                            rhs=codes.bitcast(FP8X4),
+                            rhs_scale=scales,
+                            start=False,
+                            stop=(a == PASSES - 1),
+                        )
+                    y2 = ring.tile([P, width], F32, name="y2", tag="y2", bufs=3)
+                    nc.scalar.copy(out=y2[:], in_=acc[:, width:])
+                    nc.vector.scalar_tensor_tensor(
+                        result[:, n, :], acc[:, :width], bias_sb[:, n : n + 1], y2[:], ALU.add, ALU.max
+                    )
+                nc.sync.dma_start(out=out_by_tile[:, :, lo:hi], in_=result[:])
+                lo = hi

@@ -35,64 +35,69 @@ def tile_list_duct_mode_features_kernel(
         keep = ctx.enter_context(tc.tile_pool(name="keep", bufs=1))
         ring = ctx.enter_context(tc.tile_pool(name="ring", bufs=2))
 
-        def load_scale_rows(queue, plane, rows):
+        def load_scale_rows(queues, plane, rows):
             by_r = rows.rearrange("a (q r) c -> r q a c", r=4)
-            for r in range(4):
+            for r, queue in enumerate(queues):
                 queue.dma_start(out=plane[r:P:32, :, :].bitcast(I32), in_=by_r[r].bitcast(I32))
 
         idx1 = keep.tile([P, S // 16], U16, name="idx1")
         idx2 = keep.tile([P, S // 16], U16, name="idx2")
         idx3 = keep.tile([P, M // 16], U16, name="idx3")
         nc.sync.dma_start(idx1[:], offs)
-        w1_raw = keep.tile([P, 2 * H], U8, name="w1_raw", tag="w1_then_wgs")
-        nc.sync.dma_start(out=w1_raw[:].bitcast(I32), in_=w1_words[0].bitcast(I32))
         nc.sync.dma_start(idx2[:], offs2)
         nc.sync.dma_start(idx3[:], offs3)
+        w1_raw = keep.tile([P, 2 * H], U8, name="w1_raw", tag="w1_then_wgs")
+        nc.sync.dma_start(out=w1_raw[:].bitcast(I32), in_=w1_words[0].bitcast(I32))
+        table = keep.tile([P, T], U32, name="table")
+        nc.sync.dma_start(out=table[:].bitcast(I32), in_=tab_words[0].rearrange("p t i -> p (t i)").bitcast(I32))
 
         w2_by_pass = w2.rearrange("(p j) (b c) -> b p j c", j=PACK, b=PASSES)
 
         def load_w2(b):
-            raw = keep.tile([P, PACK, K_PASS], F32, name="w2_raw%d" % b, tag="weights_raw")
+            raw = keep.tile([P, PACK, K_PASS], F32, name="w2_raw%d" % b, tag="weights_raw", align_bytes=64)
             nc.sync.dma_start(out=raw[:], in_=w2_by_pass[b])
             return raw
 
         w2_raw = load_w2(0)
-        table = keep.tile([P, T], U32, name="table")
-        nc.sync.dma_start(out=table[:].bitcast(I32), in_=tab_words[0].rearrange("p t i -> p (t i)").bitcast(I32))
 
-        table_s = keep.tile([P, T], U8, name="table_s")
+        table_s = keep.tile([P, T], U8, name="table_s", tag="v_c0", align_bytes=64)
+        w1s_raw = keep.tile([P, H], U8, name="w1s_raw", tag="v_c1", align_bytes=64)
+        nc.vector.memset(w1s_raw[:].bitcast(I32), 0)
         nc.vector.memset(table_s[:].bitcast(I32), 0)
-        load_scale_rows(nc.scalar, table_s[:].rearrange("p (a c) -> p a c", a=1), tab_scales)
+        load_scale_rows([nc.scalar] * 4, table_s[:].rearrange("p (a c) -> p a c", a=1), tab_scales)
+        load_scale_rows(
+            [nc.gpsimd, nc.gpsimd, nc.scalar, nc.scalar], w1s_raw[:].rearrange("p (a c) -> p a c", a=1), w1_scales
+        )
 
-        w1s_raw = keep.tile([P, H], U8, name="w1s_raw", tag="w1s_then_flow0", align_bytes=64)
-        nc.gpsimd.memset(w1s_raw[:].bitcast(I32), 0)
-        load_scale_rows(nc.gpsimd, w1s_raw[:].rearrange("p (a c) -> p a c", a=1), w1_scales)
+        def new_page(engine, t, tag):
+            page = keep.tile([P, T2], F32, name="page%d" % t, tag=tag, align_bytes=64)
+            engine.memset(page[:], 0.0)
+            return page
 
-        pages = [keep.tile([P, T2], F32, name="page%d" % t) for t in range(PACK)]
-        for t in range(PACK):
-            (nc.vector if t < 2 else nc.gpsimd).memset(pages[t][:], 0.0)
-
-        liner_sb = keep.tile([P, PASSES, PACK], F32, name="liner_sb")
-        nc.gpsimd.dma_start(out=liner_sb[:], in_=liner.rearrange("(b p t) -> p b t", b=PASSES, t=PACK))
-        bias_sb = keep.tile([P, N_TILES], F32, name="bias_sb")
-        with nc.allow_non_contiguous_dma(reason="one bias value for each partition and output tile"):
-            nc.gpsimd.dma_start(out=bias_sb[:], in_=bias.rearrange("(n p) -> p n", p=P))
-        w4_s = keep.tile([P, PASSES, N], U8, name="w4_s", align_bytes=64)
-        nc.gpsimd.memset(w4_s[:].rearrange("p a c -> p (a c)").bitcast(I32), 0)
-        load_scale_rows(nc.gpsimd, w4_s[:], w4_scales)
+        pages = [new_page(nc.vector, t, "page%d" % t) for t in range(2)]
 
         w1_c = keep.tile([P, 2 * H], U8, name="w1_c", align_bytes=64)
         nc.vector.tensor_copy(
-            out=w1_c[:].rearrange("p (b t q e) -> p b t q e", b=PASSES, t=PACK, e=2),
-            in_=w1_raw[:].rearrange("p (b q t e) -> p b t q e", b=PASSES, t=PACK, e=2),
+            out=w1_c[:].bitcast(U16).rearrange("p (b t q) -> p b t q", b=PASSES, t=PACK),
+            in_=w1_raw[:].bitcast(U16).rearrange("p (b q t) -> p b t q", b=PASSES, t=PACK),
         )
+        vectors = keep.tile([P, S + 16], F32, name="vectors", tag="w1_then_wgs")
+        wgs_sb = vectors[:, 0:S]
+        nc.sync.dma_start(out=wgs_sb, in_=wgs)
         w1_s = keep.tile([P, H], U8, name="w1_s", align_bytes=64)
         nc.vector.tensor_copy(
             out=w1_s[:].rearrange("p (b t q) -> p b t q", b=PASSES, t=PACK),
             in_=w1s_raw[:].rearrange("p (b q t) -> p b t q", b=PASSES, t=PACK),
         )
-        wgs_sb = keep.tile([P, S], F32, name="wgs_sb", tag="w1_then_wgs")
-        nc.sync.dma_start(out=wgs_sb[:], in_=wgs)
+
+        liner_sb = vectors[:, S : S + 8]
+        bias_sb = vectors[:, S + 8 : S + 8 + N_TILES]
+        nc.sync.dma_start(
+            out=liner_sb.rearrange("p (b t) -> p b t", b=PASSES),
+            in_=liner.rearrange("(b p t) -> p b t", b=PASSES, t=PACK),
+        )
+        with nc.allow_non_contiguous_dma(reason="one bias value for each partition and output tile"):
+            nc.sync.dma_start(out=bias_sb, in_=bias.rearrange("(n p) -> p n", p=P))
 
         flow_by_pass = flow.rearrange("(b p t) m -> b p t m", b=PASSES, t=PACK)
 
@@ -103,7 +108,7 @@ def tile_list_duct_mode_features_kernel(
 
         def add_liner(rows, b):
             for t in range(PACK):
-                nc.scalar.activation(rows[:, t, :], rows[:, t, :], ACT.Identity, bias=liner_sb[:, b, t : t + 1])
+                nc.scalar.activation(rows[:, t, :], rows[:, t, :], ACT.Identity, bias=liner_sb[:, PACK * b + t : PACK * b + t + 1])
 
         def quantize(width, rounded, name):
             codes = keep.tile([P, width], U32, name=name + "_c", align_bytes=64)
@@ -111,44 +116,42 @@ def tile_list_duct_mode_features_kernel(
             nc.vector.quantize_mx(out=codes[:].bitcast(FP8X4), scales=scales[:], in_=rounded)
             return codes, scales
 
-        def quantize_w2(raw, b, tag):
-            rounded = keep.tile([P, PACK * K_PASS], BF16, name="w2_bf%d" % b, tag=tag, align_bytes=64)
+        def quantize_w2(raw, b, t0, t1, tag):
+            count = t1 - t0
+            rounded = keep.tile([P, count * K_PASS], BF16, name="w2_bf%d_%d" % (b, t0), tag=tag, align_bytes=64)
             nc.scalar.copy(
-                out=rounded[:].rearrange("p (t q j) -> p q j t", t=PACK, j=PACK),
-                in_=raw[:].rearrange("p j (q t) -> p q j t", t=PACK),
+                out=rounded[:].rearrange("p (t q j) -> p q j t", t=count, j=PACK),
+                in_=raw[:].rearrange("p j (q t) -> p q j t", t=PACK)[:, :, :, t0:t1],
             )
-            return quantize(K_PASS, rounded[:], "w2q%d" % b)
+            codes, scales = quantize(count * P, rounded[:], "w2q%d_%d" % (b, t0))
+            return [(codes[:, i * P : (i + 1) * P], scales[:, i * P : (i + 1) * P]) for i in range(count)]
 
-        def round_and_quantize(planes, width, name):
-            rounded = ring.tile([P, PACK * width], BF16, name="rounded", tag="rounded", align_bytes=64)
+        def round_and_quantize(planes, width, name, pool, tag):
+            rounded = pool.tile([P, PACK * width], BF16, name="rounded", tag=tag, align_bytes=64)
             nc.scalar.copy(
                 out=rounded[:].rearrange("p (c i t) -> p c t i", i=4, t=PACK),
                 in_=planes.rearrange("p t (c i) -> p c t i", i=4),
             )
             return quantize(width, rounded[:], name)
 
-        w2_q = [quantize_w2(w2_raw, 0, "w2bf_then_flow1")]
-
         v_s = keep.tile([P, S], U8, name="v_s", align_bytes=64)
         nc.vector.tensor_copy(v_s[:], table_s[:].indirect(idx1[:]))
         v_c = []
         for half in range(S // BANK):
-            words = keep.tile([P, BANK], U32, name="v_c%d" % half, align_bytes=64)
+            words = keep.tile([P, BANK], U32, name="v_c%d" % half, tag="v_c%d" % half, align_bytes=64)
             nc.vector.tensor_copy(words[:], table[:].indirect(idx1[:, half * 32 : (half + 1) * 32]))
             v_c.append(words)
 
-        flows = [load_flow(0, "w1s_then_flow0")]
-        w2_raw = load_w2(1)
-        w4_c = keep.tile([P, PASSES, N], U32, name="w4_c", align_bytes=64)
-        z0 = keep.tile([P, PACK, M], F32, name="z0")
+        w2_q = quantize_w2(w2_raw, 0, 0, 1, "w2bf_then_flow0")
+        flows = [load_flow(0, "w2bf_then_flow0")]
+        z0 = keep.tile([P, PACK, M], F32, name="z0", tag="z0_then_flow1", align_bytes=64)
         z0_q = []
         w3_q = []
 
         with tc.psum_pool(name="stage1", bufs=2) as psum1:
 
             def features(s):
-                b, t = divmod(s, PACK)
-                phase = ring.tile([P, S], F32, name="phase", tag="phase", bufs=3)
+                phase = ring.tile([P, S], F32, name="phase", tag="phase")
                 level = ring.tile([P, S], F32, name="level", tag="level")
                 for half in range(S // BANK):
                     cols = slice(half * BANK, (half + 1) * BANK)
@@ -166,8 +169,8 @@ def tile_list_duct_mode_features_kernel(
                     acc2 = psum1.tile([P, BANK], F32, name="acc2", tag="acc2")
                     nc.tensor.matmul_mx(
                         out=acc2[:],
-                        lhsT=w2_q[b][0][:, t * P : (t + 1) * P].bitcast(FP8X4),
-                        lhsT_scale=w2_q[b][1][:, t * P : (t + 1) * P],
+                        lhsT=w2_q[s][0].bitcast(FP8X4),
+                        lhsT_scale=w2_q[s][1],
                         rhs=v_c[half][:].bitcast(FP8X4),
                         rhs_scale=v_s[:, cols],
                         start=True,
@@ -176,24 +179,27 @@ def tile_list_duct_mode_features_kernel(
                     nc.scalar.activation(level[:, cols], acc2[:], ACT.Abs)
                 return phase, level
 
-            def product(pair, lo, hi):
+            def product(engine, pair, lo, hi):
                 phase, level = pair
-                nc.vector.tensor_tensor(phase[:, lo:hi], phase[:, lo:hi], level[:, lo:hi], ALU.mult)
+                engine.tensor_tensor(phase[:, lo:hi], phase[:, lo:hi], level[:, lo:hi], ALU.mult)
+                engine.tensor_tensor(phase[:, lo:hi], phase[:, lo:hi], wgs_sb[:, lo:hi], ALU.mult)
+
+            def page_of(s):
+                return pages[s % 2 if s < PACK else s - PACK]
 
             def put(pair, s, lo, hi):
-                nc.vector.tensor_tensor(
-                    pages[s % PACK][:].indirect(idx2[:, lo // 16 : hi // 16]), pair[0][:, lo:hi], wgs_sb[:, lo:hi],
-                    ALU.mult,
-                )
+                nc.vector.tensor_copy(page_of(s)[:].indirect(idx2[:, lo // 16 : hi // 16]), pair[0][:, lo:hi])
 
             def fetch(dst, b, t, lo, hi):
                 nc.vector.tensor_tensor(
-                    dst, pages[t][:].indirect(idx3[:, lo // 16 : hi // 16]), flows[b][:, t, lo:hi], ALU.add
+                    dst, page_of(PACK * b + t)[:].indirect(idx3[:, lo // 16 : hi // 16]), flows[b][:, t, lo:hi], ALU.add
                 )
 
             pair = features(0)
-            for lo in range(0, S, BANK):
-                product(pair, lo, lo + BANK)
+            w2_q.extend(quantize_w2(w2_raw, 0, 1, PACK, "w2bf_rest"))
+            w2_raw = load_w2(1)
+            product(nc.vector, pair, 0, BANK)
+            product(nc.gpsimd, pair, BANK, S)
             for s in range(PASSES * PACK):
                 nxt = None
                 if s == 0:
@@ -201,31 +207,37 @@ def tile_list_duct_mode_features_kernel(
                         put(pair, s, lo, lo + BANK)
                     add_liner(flows[0], 0)
                 if s == 2:
-                    w2_q.append(quantize_w2(w2_raw, 1, "w2bf1"))
-                    flows.append(load_flow(1, "w2bf_then_flow1"))
-                    w3_raw = keep.tile([P, PASSES, PACK, N], F32, name="w3_raw", tag="weights_raw")
+                    w2_q.extend(quantize_w2(w2_raw, 1, 0, PACK, "page2"))
+                    pages.append(new_page(nc.gpsimd, 2, "page2"))
+                    w4_s = keep.tile([P, PASSES, N], U8, name="w4_s", tag="w2bf_rest", align_bytes=64)
+                    nc.gpsimd.memset(w4_s[:].rearrange("p a c -> p (a c)").bitcast(I32), 0)
+                    load_scale_rows([nc.sync] * 4, w4_s[:], w4_scales)
+                    w3_raw = keep.tile([P, PASSES, PACK, N], F32, name="w3_raw", tag="weights_raw", align_bytes=64)
                     nc.sync.dma_start(
                         out=w3_raw[:].rearrange("p a j n -> p a (j n)"),
                         in_=w3.rearrange("(a p j) n -> p a (j n)", a=PASSES, j=PACK),
                     )
-                    nc.sync.dma_start(
-                        out=w4_c[:].bitcast(I32),
-                        in_=w4_words.rearrange("a p n i -> p a (n i)").bitcast(I32),
-                    )
                 if s + 1 < PASSES * PACK:
                     nxt = features(s + 1)
-                    product(nxt, 0, S)
+                    product(nc.gpsimd, nxt, 0, S)
                 if s > 0:
                     put(pair, s, 0, S)
                 if 1 <= s <= PACK:
                     fetch(z0[:, s - 1, :], 0, s - 1, 0, M)
                 if s == PACK:
                     for lo in range(0, M, BANK):
-                        z0_q.append(round_and_quantize(z0[:, :, lo : lo + BANK], BANK, "z0q%d" % lo))
+                        z0_q.append(round_and_quantize(z0[:, :, lo : lo + BANK], BANK, "z0q%d" % lo, ring, "rounded"))
+                    flows.append(load_flow(1, "z0_then_flow1"))
                 if s == PACK + 1:
                     add_liner(flows[1], 1)
                     for a in range(PASSES):
-                        w3_q.append(round_and_quantize(w3_raw[:, a], N, "w3q%d" % a))
+                        w3_q.append(round_and_quantize(w3_raw[:, a], N, "w3q%d" % a, keep, "page3"))
+                    pages.append(new_page(nc.gpsimd, 3, "page3"))
+                    w4_c = keep.tile([P, PASSES, N], U32, name="w4_c", tag="weights_raw", align_bytes=64)
+                    nc.sync.dma_start(
+                        out=w4_c[:].bitcast(I32),
+                        in_=w4_words.rearrange("a p n i -> p a (n i)").bitcast(I32),
+                    )
                 pair = nxt
 
         out_by_tile = out.rearrange("(n p) m -> p n m", p=P)
@@ -236,7 +248,7 @@ def tile_list_duct_mode_features_kernel(
                 z1 = ring.tile([P, PACK, width], F32, name="z1", tag="z1", bufs=3)
                 for t in range(PACK):
                     fetch(z1[:, t, :], 1, t, lo, hi)
-                z1_q = round_and_quantize(z1[:], width, "z1q%d" % lo)
+                z1_q = round_and_quantize(z1[:], width, "z1q%d" % lo, ring, "rounded")
                 zc0, zs0 = z0_q[lo // BANK]
                 z0_cols = slice(lo % BANK, lo % BANK + width)
                 moving = ((zc0[:, z0_cols], zs0[:, z0_cols]), (z1_q[0][:], z1_q[1][:]))

@@ -48,17 +48,17 @@ def tile_list_duct_mode_features_kernel(
         nc.sync.dma_start(idx3[:], offs3)
         w1_raw = keep.tile([P, 2 * H], U8, name="w1_raw", tag="w1_then_wgs")
         nc.sync.dma_start(out=w1_raw[:].bitcast(I32), in_=w1_words[0].bitcast(I32))
-        table = keep.tile([P, T], U32, name="table")
+        table = keep.tile([P, T], U32, name="table", tag="weights_raw", align_bytes=64)
         nc.sync.dma_start(out=table[:].bitcast(I32), in_=tab_words[0].rearrange("p t i -> p (t i)").bitcast(I32))
 
         w2_by_pass = w2.rearrange("(p j) (b c) -> b p j c", j=PACK, b=PASSES)
 
-        def load_w2(b):
-            raw = keep.tile([P, PACK, K_PASS], F32, name="w2_raw%d" % b, tag="weights_raw", align_bytes=64)
+        def load_w2(b, tag):
+            raw = keep.tile([P, PACK, K_PASS], F32, name="w2_raw%d" % b, tag=tag, align_bytes=64)
             nc.sync.dma_start(out=raw[:], in_=w2_by_pass[b])
             return raw
 
-        w2_raw = load_w2(0)
+        w2_raw = load_w2(0, "w2_then_w4s")
 
         table_s = keep.tile([P, T], U8, name="table_s", tag="v_c0", align_bytes=64)
         w1s_raw = keep.tile([P, H], U8, name="w1s_raw", tag="v_c1", align_bytes=64)
@@ -101,14 +101,9 @@ def tile_list_duct_mode_features_kernel(
 
         flow_by_pass = flow.rearrange("(b p t) m -> b p t m", b=PASSES, t=PACK)
 
-        def load_flow(b, tag):
-            rows = keep.tile([P, PACK, M], F32, name="flow%d" % b, tag=tag, align_bytes=64)
-            nc.sync.dma_start(out=rows[:], in_=flow_by_pass[b])
-            return rows
-
-        def add_liner(rows, b):
-            for t in range(PACK):
-                nc.scalar.activation(rows[:, t, :], rows[:, t, :], ACT.Identity, bias=liner_sb[:, PACK * b + t : PACK * b + t + 1])
+        def add_liner(b, t):
+            s = PACK * b + t
+            nc.scalar.activation(flows[b][t], flows[b][t], ACT.Identity, bias=liner_sb[:, s : s + 1])
 
         def quantize(width, rounded, name):
             codes = keep.tile([P, width], U32, name=name + "_c", align_bytes=64)
@@ -126,13 +121,16 @@ def tile_list_duct_mode_features_kernel(
             codes, scales = quantize(count * P, rounded[:], "w2q%d_%d" % (b, t0))
             return [(codes[:, i * P : (i + 1) * P], scales[:, i * P : (i + 1) * P]) for i in range(count)]
 
-        def round_and_quantize(planes, width, name, pool, tag):
+        def round_planes(planes, width, pool, tag):
             rounded = pool.tile([P, PACK * width], BF16, name="rounded", tag=tag, align_bytes=64)
             nc.scalar.copy(
                 out=rounded[:].rearrange("p (c i t) -> p c t i", i=4, t=PACK),
                 in_=planes.rearrange("p t (c i) -> p c t i", i=4),
             )
-            return quantize(width, rounded[:], name)
+            return rounded
+
+        def round_and_quantize(planes, width, name, pool, tag):
+            return quantize(width, round_planes(planes, width, pool, tag)[:], name)
 
         v_s = keep.tile([P, S], U8, name="v_s", align_bytes=64)
         nc.vector.tensor_copy(v_s[:], table_s[:].indirect(idx1[:]))
@@ -142,17 +140,30 @@ def tile_list_duct_mode_features_kernel(
             nc.vector.tensor_copy(words[:], table[:].indirect(idx1[:, half * 32 : (half + 1) * 32]))
             v_c.append(words)
 
-        w2_q = quantize_w2(w2_raw, 0, 0, 1, "w2bf_then_flow0")
-        flows = [load_flow(0, "w2bf_then_flow0")]
-        z0 = keep.tile([P, PACK, M], F32, name="z0", tag="z0_then_flow1", align_bytes=64)
-        z0_q = []
-        w3_q = []
+        w2_q = quantize_w2(w2_raw, 0, 0, 1, "flow0_0")
+        w2_raw1 = load_w2(1, "weights_raw")
+        flows = [[]]
+
+        def load_flow0(t):
+            rows = keep.tile([P, M], F32, name="flow0_%d" % t, tag="flow0_%d" % t, align_bytes=64)
+            nc.sync.dma_start(out=rows[:], in_=flow_by_pass[0, :, t, :])
+            flows[0].append(rows[:])
+
+        load_flow0(0)
+        z0 = keep.tile([P, PACK, M], F32, name="z0")
 
         with tc.psum_pool(name="stage1", bufs=2) as psum1:
 
             def features(s):
-                phase = ring.tile([P, S], F32, name="phase", tag="phase")
-                level = ring.tile([P, S], F32, name="level", tag="level")
+                if s == 0:
+                    phase = keep.tile([P, S], F32, name="phase0", tag="flow0_2", align_bytes=64)
+                    level = keep.tile([P, S], F32, name="level0", tag="flow0_3", align_bytes=64)
+                else:
+                    phase = ring.tile([P, S], F32, name="phase", tag="phase")
+                    if s in (2, 3):
+                        level = keep.tile([P, S], F32, name="level%d" % s, tag="page%d" % s, align_bytes=64)
+                    else:
+                        level = ring.tile([P, S], F32, name="level", tag="level")
                 for half in range(S // BANK):
                     cols = slice(half * BANK, (half + 1) * BANK)
                     acc1 = psum1.tile([P, BANK], F32, name="acc1", tag="acc1")
@@ -179,79 +190,99 @@ def tile_list_duct_mode_features_kernel(
                     nc.scalar.activation(level[:, cols], acc2[:], ACT.Abs)
                 return phase, level
 
-            def product(engine, pair, lo, hi):
+            def product(engine, weighted, pair, lo, hi):
                 phase, level = pair
-                engine.tensor_tensor(phase[:, lo:hi], phase[:, lo:hi], level[:, lo:hi], ALU.mult)
-                engine.tensor_tensor(phase[:, lo:hi], phase[:, lo:hi], wgs_sb[:, lo:hi], ALU.mult)
+                engine.tensor_tensor(weighted[:, lo:hi], phase[:, lo:hi], level[:, lo:hi], ALU.mult)
+                engine.tensor_tensor(weighted[:, lo:hi], weighted[:, lo:hi], wgs_sb[:, lo:hi], ALU.mult)
 
             def page_of(s):
                 return pages[s % 2 if s < PACK else s - PACK]
 
-            def put(pair, s, lo, hi):
-                nc.vector.tensor_copy(page_of(s)[:].indirect(idx2[:, lo // 16 : hi // 16]), pair[0][:, lo:hi])
+            def put(weighted, s, lo, hi):
+                nc.vector.tensor_copy(page_of(s)[:].indirect(idx2[:, lo // 16 : hi // 16]), weighted[:, lo:hi])
 
             def fetch(dst, b, t, lo, hi):
                 nc.vector.tensor_tensor(
-                    dst, page_of(PACK * b + t)[:].indirect(idx3[:, lo // 16 : hi // 16]), flows[b][:, t, lo:hi], ALU.add
+                    dst, page_of(PACK * b + t)[:].indirect(idx3[:, lo // 16 : hi // 16]), flows[b][t][:, lo:hi], ALU.add
                 )
 
+            def new_weighted(s):
+                if 2 <= s < 2 + PACK:
+                    return keep.tile([P, S], F32, name="weighted%d" % s, tag="flow0_%d" % (s - 2), align_bytes=64)
+                return ring.tile([P, S], F32, name="weighted", tag="weighted", align_bytes=64)
+
             pair = features(0)
-            w2_q.extend(quantize_w2(w2_raw, 0, 1, PACK, "w2bf_rest"))
-            w2_raw = load_w2(1)
-            product(nc.vector, pair, 0, BANK)
-            product(nc.gpsimd, pair, BANK, S)
+            w2_q.extend(quantize_w2(w2_raw, 0, 1, PACK, "flow0_1"))
+            load_flow0(1)
+            now = new_weighted(0)
+            product(nc.vector, now, pair, 0, BANK)
+            product(nc.gpsimd, now, pair, BANK, S)
+            load_flow0(2)
+            load_flow0(3)
             for s in range(PASSES * PACK):
                 nxt = None
                 if s == 0:
                     for lo in range(0, S, BANK):
-                        put(pair, s, lo, lo + BANK)
-                    add_liner(flows[0], 0)
-                if s == 2:
-                    w2_q.extend(quantize_w2(w2_raw, 1, 0, PACK, "page2"))
-                    pages.append(new_page(nc.gpsimd, 2, "page2"))
-                    w4_s = keep.tile([P, PASSES, N], U8, name="w4_s", tag="w2bf_rest", align_bytes=64)
-                    nc.gpsimd.memset(w4_s[:].rearrange("p a c -> p (a c)").bitcast(I32), 0)
+                        put(now, s, lo, lo + BANK)
+                if s + 1 < PASSES * PACK:
+                    nxt = new_weighted(s + 1)
+                    product(nc.gpsimd, nxt, features(s + 1), 0, S)
+                    if s + 1 in (2, 3):
+                        pages.append(new_page(nc.gpsimd, s + 1, "page%d" % (s + 1)))
+                if s > 0:
+                    put(now, s, 0, S)
+                if s < PACK:
+                    add_liner(0, s)
+                    fetch(z0[:, s, :], 0, s, 0, M)
+                if s == 1:
+                    w2_q.extend(quantize_w2(w2_raw1, 1, 0, PACK, "w2bf1"))
+                    flow1 = keep.tile([P, PACK, M], F32, name="flow1", tag="w2bf1", align_bytes=64)
+                    nc.sync.dma_start(out=flow1[:], in_=flow_by_pass[1])
+                    flows.append([flow1[:, t, :] for t in range(PACK)])
+                    w4_s = keep.tile([P, PASSES, N], U8, name="w4_s", tag="w2_then_w4s", align_bytes=64)
+                    nc.vector.memset(w4_s[:].rearrange("p a c -> p (a c)").bitcast(I32), 0)
                     load_scale_rows([nc.sync] * 4, w4_s[:], w4_scales)
                     w3_raw = keep.tile([P, PASSES, PACK, N], F32, name="w3_raw", tag="weights_raw", align_bytes=64)
                     nc.sync.dma_start(
                         out=w3_raw[:].rearrange("p a j n -> p a (j n)"),
                         in_=w3.rearrange("(a p j) n -> p a (j n)", a=PASSES, j=PACK),
                     )
-                if s + 1 < PASSES * PACK:
-                    nxt = features(s + 1)
-                    product(nc.gpsimd, nxt, 0, S)
-                if s > 0:
-                    put(pair, s, 0, S)
-                if 1 <= s <= PACK:
-                    fetch(z0[:, s - 1, :], 0, s - 1, 0, M)
-                if s == PACK:
-                    for lo in range(0, M, BANK):
-                        z0_q.append(round_and_quantize(z0[:, :, lo : lo + BANK], BANK, "z0q%d" % lo, ring, "rounded"))
-                    flows.append(load_flow(1, "z0_then_flow1"))
-                if s == PACK + 1:
-                    add_liner(flows[1], 1)
+                if s == PASSES * PACK - 2:
+                    late_bf = []
                     for a in range(PASSES):
-                        w3_q.append(round_and_quantize(w3_raw[:, a], N, "w3q%d" % a, keep, "page3"))
-                    pages.append(new_page(nc.gpsimd, 3, "page3"))
+                        late_bf.append((N, round_planes(w3_raw[:, a], N, keep, "w3bf%d" % a)))
                     w4_c = keep.tile([P, PASSES, N], U32, name="w4_c", tag="weights_raw", align_bytes=64)
                     nc.sync.dma_start(
                         out=w4_c[:].bitcast(I32),
                         in_=w4_words.rearrange("a p n i -> p a (n i)").bitcast(I32),
                     )
-                pair = nxt
+                    for t in range(PACK):
+                        add_liner(1, t)
+                    for half in range(M // BANK):
+                        planes = z0[:, :, half * BANK : (half + 1) * BANK]
+                        late_bf.append((BANK, round_planes(planes, BANK, keep, "v_c%d" % half)))
+                    late_c = ring.tile([P, PASSES * N + M], U32, name="late_c", tag="weighted", align_bytes=64)
+                    late_s = keep.tile([P, PASSES * N + M], U8, name="late_s", align_bytes=64)
+                    lo = 0
+                    for width, rounded in late_bf:
+                        cols = slice(lo, lo + width)
+                        nc.vector.quantize_mx(out=late_c[:, cols].bitcast(FP8X4), scales=late_s[:, cols], in_=rounded[:])
+                        lo += width
+                now = nxt
 
+        w3_q = [(late_c[:, a * N : (a + 1) * N], late_s[:, a * N : (a + 1) * N]) for a in range(PASSES)]
+        z0_c = late_c[:, PASSES * N :]
+        z0_s = late_s[:, PASSES * N :]
         out_by_tile = out.rearrange("(n p) m -> p n m", p=P)
         with tc.psum_pool(name="stage2", bufs=8) as psum2:
             lo = 0
-            for width in LAST_CHUNKS:
+            for c, width in enumerate(LAST_CHUNKS):
                 hi = lo + width
-                z1 = ring.tile([P, PACK, width], F32, name="z1", tag="z1", bufs=3)
+                z1 = keep.tile([P, PACK, width], F32, name="z1_%d" % c, tag="tail%d" % (c % 3), align_bytes=64)
                 for t in range(PACK):
                     fetch(z1[:, t, :], 1, t, lo, hi)
-                z1_q = round_and_quantize(z1[:], width, "z1q%d" % lo, ring, "rounded")
-                zc0, zs0 = z0_q[lo // BANK]
-                z0_cols = slice(lo % BANK, lo % BANK + width)
-                moving = ((zc0[:, z0_cols], zs0[:, z0_cols]), (z1_q[0][:], z1_q[1][:]))
+                z1_q = round_and_quantize(z1[:], width, "z1q%d" % lo, keep, "tail%d" % ((c + 2) % 3))
+                moving = ((z0_c[:, lo:hi], z0_s[:, lo:hi]), (z1_q[0][:], z1_q[1][:]))
                 result = ring.tile([P, N_TILES, width], F32, name="result", tag="result", bufs=3)
                 for n in range(N_TILES):
                     rows = slice(n * P, (n + 1) * P)

@@ -22,6 +22,8 @@ K_PASS = P * PACK
 BANK = 512
 PASSES = H // K_PASS
 N_TILES = N // P
+HALVES = ((0, 512), (512, 1024))
+FIRST_PIECES = ((0, 256), (256, 512), (512, 1024))
 LAST_CHUNKS = (256, 256, 256, 128, 128)
 
 
@@ -35,19 +37,25 @@ def tile_list_duct_mode_features_kernel(
         keep = ctx.enter_context(tc.tile_pool(name="keep", bufs=1))
         ring = ctx.enter_context(tc.tile_pool(name="ring", bufs=2))
 
-        def load_scale_rows(queues, plane, rows):
+        def load_scale_rows(plane, rows):
             by_r = rows.rearrange("a (q r) c -> r q a c", r=4)
-            for r, queue in enumerate(queues):
-                queue.dma_start(out=plane[r:P:32, :, :].bitcast(I32), in_=by_r[r].bitcast(I32))
+            for r in range(4):
+                nc.sync.dma_start(out=plane[r:P:32, :, :].bitcast(I32), in_=by_r[r].bitcast(I32))
 
         idx1 = keep.tile([P, S // 16], U16, name="idx1")
         idx2 = keep.tile([P, S // 16], U16, name="idx2")
         idx3 = keep.tile([P, M // 16], U16, name="idx3")
+        w1_raw = keep.tile([P, 2 * H], U8, name="w1_raw", tag="w1_then_wgs")
+        w1s_raw = keep.tile([P, H], U8, name="w1s_raw", tag="v_c1", align_bytes=64)
+        table_s = keep.tile([P, T], U8, name="table_s", tag="v_c0", align_bytes=64)
+        nc.gpsimd.memset(w1s_raw[:].bitcast(I32), 0)
+        nc.vector.memset(table_s[:].bitcast(I32), 0)
         nc.sync.dma_start(idx1[:], offs)
+        nc.sync.dma_start(out=w1_raw[:].bitcast(I32), in_=w1_words[0].bitcast(I32))
+        load_scale_rows(w1s_raw[:].rearrange("p (a c) -> p a c", a=1), w1_scales)
+        load_scale_rows(table_s[:].rearrange("p (a c) -> p a c", a=1), tab_scales)
         nc.sync.dma_start(idx2[:], offs2)
         nc.sync.dma_start(idx3[:], offs3)
-        w1_raw = keep.tile([P, 2 * H], U8, name="w1_raw", tag="w1_then_wgs")
-        nc.sync.dma_start(out=w1_raw[:].bitcast(I32), in_=w1_words[0].bitcast(I32))
         table = keep.tile([P, T], U32, name="table", tag="weights_raw", align_bytes=64)
         nc.sync.dma_start(out=table[:].bitcast(I32), in_=tab_words[0].rearrange("p t i -> p (t i)").bitcast(I32))
 
@@ -59,15 +67,6 @@ def tile_list_duct_mode_features_kernel(
             return raw
 
         w2_raw = load_w2(0, "w2_then_w4s")
-
-        table_s = keep.tile([P, T], U8, name="table_s", tag="v_c0", align_bytes=64)
-        w1s_raw = keep.tile([P, H], U8, name="w1s_raw", tag="v_c1", align_bytes=64)
-        nc.vector.memset(w1s_raw[:].bitcast(I32), 0)
-        nc.vector.memset(table_s[:].bitcast(I32), 0)
-        load_scale_rows([nc.scalar] * 4, table_s[:].rearrange("p (a c) -> p a c", a=1), tab_scales)
-        load_scale_rows(
-            [nc.gpsimd, nc.gpsimd, nc.scalar, nc.scalar], w1s_raw[:].rearrange("p (a c) -> p a c", a=1), w1_scales
-        )
 
         def new_page(engine, t, tag):
             page = keep.tile([P, T2], F32, name="page%d" % t, tag=tag, align_bytes=64)
@@ -111,10 +110,10 @@ def tile_list_duct_mode_features_kernel(
             nc.vector.quantize_mx(out=codes[:].bitcast(FP8X4), scales=scales[:], in_=rounded)
             return codes, scales
 
-        def quantize_w2(raw, b, t0, t1, tag):
+        def quantize_w2(copy, raw, b, t0, t1, tag):
             count = t1 - t0
             rounded = keep.tile([P, count * K_PASS], BF16, name="w2_bf%d_%d" % (b, t0), tag=tag, align_bytes=64)
-            nc.scalar.copy(
+            copy(
                 out=rounded[:].rearrange("p (t q j) -> p q j t", t=count, j=PACK),
                 in_=raw[:].rearrange("p j (q t) -> p q j t", t=PACK)[:, :, :, t0:t1],
             )
@@ -140,7 +139,7 @@ def tile_list_duct_mode_features_kernel(
             nc.vector.tensor_copy(words[:], table[:].indirect(idx1[:, half * 32 : (half + 1) * 32]))
             v_c.append(words)
 
-        w2_q = quantize_w2(w2_raw, 0, 0, 1, "flow0_0")
+        w2_q = quantize_w2(nc.vector.tensor_copy, w2_raw, 0, 0, 1, "flow0_0")
         w2_raw1 = load_w2(1, "weights_raw")
         flows = [[]]
 
@@ -154,7 +153,7 @@ def tile_list_duct_mode_features_kernel(
 
         with tc.psum_pool(name="stage1", bufs=2) as psum1:
 
-            def features(s):
+            def features(s, pieces):
                 if s == 0:
                     phase = keep.tile([P, S], F32, name="phase0", tag="flow0_2", align_bytes=64)
                     level = keep.tile([P, S], F32, name="level0", tag="flow0_3", align_bytes=64)
@@ -164,25 +163,26 @@ def tile_list_duct_mode_features_kernel(
                         level = keep.tile([P, S], F32, name="level%d" % s, tag="page%d" % s, align_bytes=64)
                     else:
                         level = ring.tile([P, S], F32, name="level", tag="level")
-                for half in range(S // BANK):
-                    cols = slice(half * BANK, (half + 1) * BANK)
-                    acc1 = psum1.tile([P, BANK], F32, name="acc1", tag="acc1")
+                for lo, hi in pieces:
+                    cols = slice(lo, hi)
+                    words = v_c[lo // BANK][:, lo % BANK : lo % BANK + hi - lo]
+                    acc1 = psum1.tile([P, hi - lo], F32, name="acc1", tag="acc1")
                     nc.tensor.matmul_mx(
                         out=acc1[:],
                         lhsT=w1_c[:, s * 2 * P : (s + 1) * 2 * P].bitcast(FP4X4),
                         lhsT_scale=w1_s[:, s * P : (s + 1) * P],
-                        rhs=v_c[half][:].bitcast(FP8X4),
+                        rhs=words.bitcast(FP8X4),
                         rhs_scale=v_s[:, cols],
                         start=True,
                         stop=True,
                     )
                     nc.scalar.activation(phase[:, cols], acc1[:], ACT.Tanh)
-                    acc2 = psum1.tile([P, BANK], F32, name="acc2", tag="acc2")
+                    acc2 = psum1.tile([P, hi - lo], F32, name="acc2", tag="acc2")
                     nc.tensor.matmul_mx(
                         out=acc2[:],
                         lhsT=w2_q[s][0].bitcast(FP8X4),
                         lhsT_scale=w2_q[s][1],
-                        rhs=v_c[half][:].bitcast(FP8X4),
+                        rhs=words.bitcast(FP8X4),
                         rhs_scale=v_s[:, cols],
                         start=True,
                         stop=True,
@@ -211,22 +211,20 @@ def tile_list_duct_mode_features_kernel(
                     return keep.tile([P, S], F32, name="weighted%d" % s, tag="flow0_%d" % (s - 2), align_bytes=64)
                 return ring.tile([P, S], F32, name="weighted", tag="weighted", align_bytes=64)
 
-            pair = features(0)
-            w2_q.extend(quantize_w2(w2_raw, 0, 1, PACK, "flow0_1"))
+            pair = features(0, FIRST_PIECES)
+            w2_q.extend(quantize_w2(nc.scalar.copy, w2_raw, 0, 1, PACK, "flow0_1"))
             load_flow0(1)
             now = new_weighted(0)
-            product(nc.vector, now, pair, 0, BANK)
-            product(nc.gpsimd, now, pair, BANK, S)
+            for lo, hi in FIRST_PIECES:
+                product(nc.vector, now, pair, lo, hi)
+                put(now, 0, lo, hi)
             load_flow0(2)
             load_flow0(3)
             for s in range(PASSES * PACK):
                 nxt = None
-                if s == 0:
-                    for lo in range(0, S, BANK):
-                        put(now, s, lo, lo + BANK)
                 if s + 1 < PASSES * PACK:
                     nxt = new_weighted(s + 1)
-                    product(nc.gpsimd, nxt, features(s + 1), 0, S)
+                    product(nc.gpsimd, nxt, features(s + 1, HALVES), 0, S)
                     if s + 1 in (2, 3):
                         pages.append(new_page(nc.gpsimd, s + 1, "page%d" % (s + 1)))
                 if s > 0:
@@ -235,13 +233,13 @@ def tile_list_duct_mode_features_kernel(
                     add_liner(0, s)
                     fetch(z0[:, s, :], 0, s, 0, M)
                 if s == 1:
-                    w2_q.extend(quantize_w2(w2_raw1, 1, 0, PACK, "w2bf1"))
+                    w2_q.extend(quantize_w2(nc.scalar.copy, w2_raw1, 1, 0, PACK, "w2bf1"))
                     flow1 = keep.tile([P, PACK, M], F32, name="flow1", tag="w2bf1", align_bytes=64)
                     nc.sync.dma_start(out=flow1[:], in_=flow_by_pass[1])
                     flows.append([flow1[:, t, :] for t in range(PACK)])
                     w4_s = keep.tile([P, PASSES, N], U8, name="w4_s", tag="w2_then_w4s", align_bytes=64)
                     nc.vector.memset(w4_s[:].rearrange("p a c -> p (a c)").bitcast(I32), 0)
-                    load_scale_rows([nc.sync] * 4, w4_s[:], w4_scales)
+                    load_scale_rows(w4_s[:], w4_scales)
                     w3_raw = keep.tile([P, PASSES, PACK, N], F32, name="w3_raw", tag="weights_raw", align_bytes=64)
                     nc.sync.dma_start(
                         out=w3_raw[:].rearrange("p a j n -> p a (j n)"),

@@ -19,12 +19,17 @@ ALU = mybir.AluOpType
 P = 128
 PACK = 4
 K_PASS = P * PACK
+GROUP = 16
 BANK = 512
+ALIGN = 64
 PASSES = H // K_PASS
+SLICES = PASSES * PACK
 N_TILES = N // P
+EARLY_PAGES = 2
 HALVES = ((0, 512), (512, 1024))
 FIRST_PIECES = ((0, 256), (256, 512), (512, 1024))
-LAST_CHUNKS = (256, 256, 256, 128, 128)
+CHUNKS = (256, 256, 256, 128, 128)
+CHUNK_SLOTS = 3
 
 
 def tile_list_duct_mode_features_kernel(
@@ -37,17 +42,17 @@ def tile_list_duct_mode_features_kernel(
         keep = ctx.enter_context(tc.tile_pool(name="keep", bufs=1))
         ring = ctx.enter_context(tc.tile_pool(name="ring", bufs=2))
 
-        def load_scale_rows(plane, rows):
-            by_r = rows.rearrange("a (q r) c -> r q a c", r=4)
-            for r in range(4):
-                nc.sync.dma_start(out=plane[r:P:32, :, :].bitcast(I32), in_=by_r[r].bitcast(I32))
+        def load_scale_rows(scales, rows):
+            by_i = rows.rearrange("a (quadrant i) c -> i quadrant a c", i=4)
+            for i in range(4):
+                nc.sync.dma_start(out=scales[i:P:32, :, :].bitcast(I32), in_=by_i[i].bitcast(I32))
 
-        idx1 = keep.tile([P, S // 16], U16, name="idx1")
-        idx2 = keep.tile([P, S // 16], U16, name="idx2")
-        idx3 = keep.tile([P, M // 16], U16, name="idx3")
-        w1_raw = keep.tile([P, 2 * H], U8, name="w1_raw", tag="w1_then_wgs")
-        w1s_raw = keep.tile([P, H], U8, name="w1s_raw", tag="v_c1", align_bytes=64)
-        table_s = keep.tile([P, T], U8, name="table_s", tag="v_c0", align_bytes=64)
+        idx1 = keep.tile([P, S // GROUP], U16, name="idx1")
+        idx2 = keep.tile([P, S // GROUP], U16, name="idx2")
+        idx3 = keep.tile([P, M // GROUP], U16, name="idx3")
+        w1_raw = keep.tile([P, 2 * H], U8, name="w1_raw", tag="w1_then_vectors")
+        w1s_raw = keep.tile([P, H], U8, name="w1s_raw", tag="v_c1", align_bytes=ALIGN)
+        table_s = keep.tile([P, T], U8, name="table_s", tag="v_c0", align_bytes=ALIGN)
         nc.gpsimd.memset(w1s_raw[:].bitcast(I32), 0)
         nc.vector.memset(table_s[:].bitcast(I32), 0)
         nc.sync.dma_start(idx1[:], offs)
@@ -56,41 +61,41 @@ def tile_list_duct_mode_features_kernel(
         load_scale_rows(table_s[:].rearrange("p (a c) -> p a c", a=1), tab_scales)
         nc.sync.dma_start(idx2[:], offs2)
         nc.sync.dma_start(idx3[:], offs3)
-        table = keep.tile([P, T], U32, name="table", tag="weights_raw", align_bytes=64)
+        table = keep.tile([P, T], U32, name="table", tag="weights_raw", align_bytes=ALIGN)
         nc.sync.dma_start(out=table[:].bitcast(I32), in_=tab_words[0].rearrange("p t i -> p (t i)").bitcast(I32))
 
-        w2_by_pass = w2.rearrange("(p j) (b c) -> b p j c", j=PACK, b=PASSES)
+        w2_by_half = w2.rearrange("(p j) (b c) -> b p j c", j=PACK, b=PASSES)
 
         def load_w2(b, tag):
-            raw = keep.tile([P, PACK, K_PASS], F32, name="w2_raw%d" % b, tag=tag, align_bytes=64)
-            nc.sync.dma_start(out=raw[:], in_=w2_by_pass[b])
+            raw = keep.tile([P, PACK, K_PASS], F32, name="w2_raw%d" % b, tag=tag, align_bytes=ALIGN)
+            nc.sync.dma_start(out=raw[:], in_=w2_by_half[b])
             return raw
 
-        w2_raw = load_w2(0, "w2_then_w4s")
+        w2_raw0 = load_w2(0, "w2_then_w4s")
 
-        def new_page(engine, t, tag):
-            page = keep.tile([P, T2], F32, name="page%d" % t, tag=tag, align_bytes=64)
+        def new_page(engine, number):
+            page = keep.tile([P, T2], F32, name="page%d" % number, tag="page%d" % number, align_bytes=ALIGN)
             engine.memset(page[:], 0.0)
             return page
 
-        pages = [new_page(nc.vector, t, "page%d" % t) for t in range(2)]
+        pages = [new_page(nc.vector, number) for number in range(EARLY_PAGES)]
 
-        w1_c = keep.tile([P, 2 * H], U8, name="w1_c", align_bytes=64)
+        w1_c = keep.tile([P, 2 * H], U8, name="w1_c", align_bytes=ALIGN)
         nc.vector.tensor_copy(
             out=w1_c[:].bitcast(U16).rearrange("p (b t q) -> p b t q", b=PASSES, t=PACK),
             in_=w1_raw[:].bitcast(U16).rearrange("p (b q t) -> p b t q", b=PASSES, t=PACK),
         )
-        vectors = keep.tile([P, S + 16], F32, name="vectors", tag="w1_then_wgs")
+        vectors = keep.tile([P, S + 2 * SLICES], F32, name="vectors", tag="w1_then_vectors")
         wgs_sb = vectors[:, 0:S]
         nc.sync.dma_start(out=wgs_sb, in_=wgs)
-        w1_s = keep.tile([P, H], U8, name="w1_s", align_bytes=64)
+        w1_s = keep.tile([P, H], U8, name="w1_s", align_bytes=ALIGN)
         nc.vector.tensor_copy(
             out=w1_s[:].rearrange("p (b t q) -> p b t q", b=PASSES, t=PACK),
             in_=w1s_raw[:].rearrange("p (b q t) -> p b t q", b=PASSES, t=PACK),
         )
 
-        liner_sb = vectors[:, S : S + 8]
-        bias_sb = vectors[:, S + 8 : S + 8 + N_TILES]
+        liner_sb = vectors[:, S : S + SLICES]
+        bias_sb = vectors[:, S + SLICES : S + SLICES + N_TILES]
         nc.sync.dma_start(
             out=liner_sb.rearrange("p (b t) -> p b t", b=PASSES),
             in_=liner.rearrange("(b p t) -> p b t", b=PASSES, t=PACK),
@@ -99,20 +104,20 @@ def tile_list_duct_mode_features_kernel(
             nc.sync.dma_start(out=bias_sb, in_=bias.rearrange("(n p) -> p n", p=P))
 
         flow_by_pass = flow.rearrange("(b p t) m -> b p t m", b=PASSES, t=PACK)
+        flows = []
 
-        def add_liner(b, t):
-            s = PACK * b + t
-            nc.scalar.activation(flows[b][t], flows[b][t], ACT.Identity, bias=liner_sb[:, s : s + 1])
+        def add_liner(s):
+            nc.scalar.activation(flows[s], flows[s], ACT.Identity, bias=liner_sb[:, s : s + 1])
 
         def quantize(width, rounded, name):
-            codes = keep.tile([P, width], U32, name=name + "_c", align_bytes=64)
-            scales = keep.tile([P, width], U8, name=name + "_s", align_bytes=64)
+            codes = keep.tile([P, width], U32, name=name + "_c", align_bytes=ALIGN)
+            scales = keep.tile([P, width], U8, name=name + "_s", align_bytes=ALIGN)
             nc.vector.quantize_mx(out=codes[:].bitcast(FP8X4), scales=scales[:], in_=rounded)
             return codes, scales
 
         def quantize_w2(copy, raw, b, t0, t1, tag):
             count = t1 - t0
-            rounded = keep.tile([P, count * K_PASS], BF16, name="w2_bf%d_%d" % (b, t0), tag=tag, align_bytes=64)
+            rounded = keep.tile([P, count * K_PASS], BF16, name="w2_bf%d_%d" % (b, t0), tag=tag, align_bytes=ALIGN)
             copy(
                 out=rounded[:].rearrange("p (t q j) -> p q j t", t=count, j=PACK),
                 in_=raw[:].rearrange("p j (q t) -> p q j t", t=PACK)[:, :, :, t0:t1],
@@ -120,47 +125,50 @@ def tile_list_duct_mode_features_kernel(
             codes, scales = quantize(count * P, rounded[:], "w2q%d_%d" % (b, t0))
             return [(codes[:, i * P : (i + 1) * P], scales[:, i * P : (i + 1) * P]) for i in range(count)]
 
-        def round_planes(planes, width, pool, tag):
-            rounded = pool.tile([P, PACK * width], BF16, name="rounded", tag=tag, align_bytes=64)
+        def round_rows(rows, width, tag):
+            rounded = keep.tile([P, PACK * width], BF16, name="rounded", tag=tag, align_bytes=ALIGN)
             nc.scalar.copy(
                 out=rounded[:].rearrange("p (c i t) -> p c t i", i=4, t=PACK),
-                in_=planes.rearrange("p t (c i) -> p c t i", i=4),
+                in_=rows.rearrange("p t (c i) -> p c t i", i=4),
             )
             return rounded
 
-        def round_and_quantize(planes, width, name, pool, tag):
-            return quantize(width, round_planes(planes, width, pool, tag)[:], name)
-
-        v_s = keep.tile([P, S], U8, name="v_s", align_bytes=64)
+        v_s = keep.tile([P, S], U8, name="v_s", align_bytes=ALIGN)
         nc.vector.tensor_copy(v_s[:], table_s[:].indirect(idx1[:]))
         v_c = []
-        for half in range(S // BANK):
-            words = keep.tile([P, BANK], U32, name="v_c%d" % half, tag="v_c%d" % half, align_bytes=64)
-            nc.vector.tensor_copy(words[:], table[:].indirect(idx1[:, half * 32 : (half + 1) * 32]))
+        for half, (lo, hi) in enumerate(HALVES):
+            words = keep.tile([P, hi - lo], U32, name="v_c%d" % half, tag="v_c%d" % half, align_bytes=ALIGN)
+            nc.vector.tensor_copy(words[:], table[:].indirect(idx1[:, lo // GROUP : hi // GROUP]))
             v_c.append(words)
 
-        w2_q = quantize_w2(nc.vector.tensor_copy, w2_raw, 0, 0, 1, "flow0_0")
+        w2_q = quantize_w2(nc.vector.tensor_copy, w2_raw0, 0, 0, 1, "flow0")
         w2_raw1 = load_w2(1, "weights_raw")
-        flows = [[]]
 
-        def load_flow0(t):
-            rows = keep.tile([P, M], F32, name="flow0_%d" % t, tag="flow0_%d" % t, align_bytes=64)
-            nc.sync.dma_start(out=rows[:], in_=flow_by_pass[0, :, t, :])
-            flows[0].append(rows[:])
+        def load_flow_slice(s):
+            rows = keep.tile([P, M], F32, name="flow%d" % s, tag="flow%d" % s, align_bytes=ALIGN)
+            nc.sync.dma_start(out=rows[:], in_=flow_by_pass[0, :, s, :])
+            flows.append(rows[:])
 
-        load_flow0(0)
+        load_flow_slice(0)
         z0 = keep.tile([P, PACK, M], F32, name="z0")
+
+        def page_of(s):
+            return pages[s % EARLY_PAGES if s < PACK else s - PACK]
+
+        def fetch(dst, s, lo, hi):
+            picked = page_of(s)[:].indirect(idx3[:, lo // GROUP : hi // GROUP])
+            nc.vector.tensor_tensor(dst, picked, flows[s][:, lo:hi], ALU.add)
 
         with tc.psum_pool(name="stage1", bufs=2) as psum1:
 
             def features(s, pieces):
                 if s == 0:
-                    phase = keep.tile([P, S], F32, name="phase0", tag="flow0_2", align_bytes=64)
-                    level = keep.tile([P, S], F32, name="level0", tag="flow0_3", align_bytes=64)
+                    phase = keep.tile([P, S], F32, name="phase0", tag="flow3", align_bytes=ALIGN)
+                    level = keep.tile([P, S], F32, name="level0", tag="flow2", align_bytes=ALIGN)
                 else:
                     phase = ring.tile([P, S], F32, name="phase", tag="phase")
-                    if s in (2, 3):
-                        level = keep.tile([P, S], F32, name="level%d" % s, tag="page%d" % s, align_bytes=64)
+                    if EARLY_PAGES <= s < PACK:
+                        level = keep.tile([P, S], F32, name="level%d" % s, tag="page%d" % s, align_bytes=ALIGN)
                     else:
                         level = ring.tile([P, S], F32, name="level", tag="level")
                 for lo, hi in pieces:
@@ -192,95 +200,96 @@ def tile_list_duct_mode_features_kernel(
 
             def product(engine, weighted, pair, lo, hi):
                 phase, level = pair
-                engine.tensor_tensor(weighted[:, lo:hi], phase[:, lo:hi], level[:, lo:hi], ALU.mult)
-                engine.tensor_tensor(weighted[:, lo:hi], weighted[:, lo:hi], wgs_sb[:, lo:hi], ALU.mult)
-
-            def page_of(s):
-                return pages[s % 2 if s < PACK else s - PACK]
+                engine.tensor_tensor(weighted[:, lo:hi], level[:, lo:hi], wgs_sb[:, lo:hi], ALU.mult)
+                engine.tensor_tensor(weighted[:, lo:hi], weighted[:, lo:hi], phase[:, lo:hi], ALU.mult)
 
             def put(weighted, s, lo, hi):
-                nc.vector.tensor_copy(page_of(s)[:].indirect(idx2[:, lo // 16 : hi // 16]), weighted[:, lo:hi])
-
-            def fetch(dst, b, t, lo, hi):
-                nc.vector.tensor_tensor(
-                    dst, page_of(PACK * b + t)[:].indirect(idx3[:, lo // 16 : hi // 16]), flows[b][t][:, lo:hi], ALU.add
-                )
+                places = page_of(s)[:].indirect(idx2[:, lo // GROUP : hi // GROUP])
+                nc.vector.tensor_copy(places, weighted[:, lo:hi])
 
             def new_weighted(s):
+                if s == 1:
+                    return keep.tile([P, S], F32, name="weighted1", tag="flow3", align_bytes=ALIGN)
                 if 2 <= s < 2 + PACK:
-                    return keep.tile([P, S], F32, name="weighted%d" % s, tag="flow0_%d" % (s - 2), align_bytes=64)
-                return ring.tile([P, S], F32, name="weighted", tag="weighted", align_bytes=64)
+                    return keep.tile([P, S], F32, name="weighted%d" % s, tag="flow%d" % (s - 2), align_bytes=ALIGN)
+                return ring.tile([P, S], F32, name="weighted", tag="weighted", align_bytes=ALIGN)
 
             pair = features(0, FIRST_PIECES)
-            w2_q.extend(quantize_w2(nc.scalar.copy, w2_raw, 0, 1, PACK, "flow0_1"))
-            load_flow0(1)
+            w2_q.extend(quantize_w2(nc.scalar.copy, w2_raw0, 0, 1, PACK, "flow1"))
+            load_flow_slice(1)
             now = new_weighted(0)
             for lo, hi in FIRST_PIECES:
                 product(nc.vector, now, pair, lo, hi)
-                put(now, 0, lo, hi)
-            load_flow0(2)
-            load_flow0(3)
-            for s in range(PASSES * PACK):
-                nxt = None
-                if s + 1 < PASSES * PACK:
-                    nxt = new_weighted(s + 1)
-                    product(nc.gpsimd, nxt, features(s + 1, HALVES), 0, S)
-                    if s + 1 in (2, 3):
-                        pages.append(new_page(nc.gpsimd, s + 1, "page%d" % (s + 1)))
+                if lo == 0:
+                    put(now, 0, lo, hi)
+            put(now, 0, FIRST_PIECES[0][1], S)
+            load_flow_slice(2)
+
+            for s in range(SLICES):
+                following = None
+                if s + 1 < SLICES:
+                    following = new_weighted(s + 1)
+                    product(nc.gpsimd, following, features(s + 1, HALVES), 0, S)
+                    if EARLY_PAGES <= s + 1 < PACK:
+                        pages.append(new_page(nc.gpsimd, s + 1))
                 if s > 0:
                     put(now, s, 0, S)
                 if s < PACK:
-                    add_liner(0, s)
-                    fetch(z0[:, s, :], 0, s, 0, M)
+                    add_liner(s)
+                    fetch(z0[:, s, :], s, 0, M)
                 if s == 1:
-                    w2_q.extend(quantize_w2(nc.scalar.copy, w2_raw1, 1, 0, PACK, "w2bf1"))
-                    flow1 = keep.tile([P, PACK, M], F32, name="flow1", tag="w2bf1", align_bytes=64)
-                    nc.sync.dma_start(out=flow1[:], in_=flow_by_pass[1])
-                    flows.append([flow1[:, t, :] for t in range(PACK)])
-                    w4_s = keep.tile([P, PASSES, N], U8, name="w4_s", tag="w2_then_w4s", align_bytes=64)
+                    load_flow_slice(3)
+                    w2_q.extend(quantize_w2(nc.scalar.copy, w2_raw1, 1, 0, PACK, "w2bf_then_flow"))
+                    flow_late = keep.tile([P, PACK, M], F32, name="flow_late", tag="w2bf_then_flow", align_bytes=ALIGN)
+                    nc.sync.dma_start(out=flow_late[:], in_=flow_by_pass[1])
+                    flows.extend(flow_late[:, t, :] for t in range(PACK))
+                    w4_s = keep.tile([P, PASSES, N], U8, name="w4_s", tag="w2_then_w4s", align_bytes=ALIGN)
                     nc.vector.memset(w4_s[:].rearrange("p a c -> p (a c)").bitcast(I32), 0)
                     load_scale_rows(w4_s[:], w4_scales)
-                    w3_raw = keep.tile([P, PASSES, PACK, N], F32, name="w3_raw", tag="weights_raw", align_bytes=64)
+                    w3_raw = keep.tile([P, PASSES, PACK, N], F32, name="w3_raw", tag="weights_raw", align_bytes=ALIGN)
                     nc.sync.dma_start(
                         out=w3_raw[:].rearrange("p a j n -> p a (j n)"),
                         in_=w3.rearrange("(a p j) n -> p a (j n)", a=PASSES, j=PACK),
                     )
-                if s == PASSES * PACK - 2:
+                if s == SLICES - 2:
                     late_bf = []
                     for a in range(PASSES):
-                        late_bf.append((N, round_planes(w3_raw[:, a], N, keep, "w3bf%d" % a)))
-                    w4_c = keep.tile([P, PASSES, N], U32, name="w4_c", tag="weights_raw", align_bytes=64)
+                        late_bf.append((N, round_rows(w3_raw[:, a], N, "w3_bf%d" % a)))
+                    w4_c = keep.tile([P, PASSES, N], U32, name="w4_c", tag="weights_raw", align_bytes=ALIGN)
                     nc.sync.dma_start(
                         out=w4_c[:].bitcast(I32),
                         in_=w4_words.rearrange("a p n i -> p a (n i)").bitcast(I32),
                     )
                     for t in range(PACK):
-                        add_liner(1, t)
-                    for half in range(M // BANK):
-                        planes = z0[:, :, half * BANK : (half + 1) * BANK]
-                        late_bf.append((BANK, round_planes(planes, BANK, keep, "v_c%d" % half)))
-                    late_c = ring.tile([P, PASSES * N + M], U32, name="late_c", tag="weighted", align_bytes=64)
-                    late_s = keep.tile([P, PASSES * N + M], U8, name="late_s", align_bytes=64)
-                    lo = 0
+                        add_liner(PACK + t)
+                    for half, (lo, hi) in enumerate(HALVES):
+                        late_bf.append((hi - lo, round_rows(z0[:, :, lo:hi], hi - lo, "v_c%d" % half)))
+                    late_c = ring.tile([P, PASSES * N + M], U32, name="late_c", tag="weighted", align_bytes=ALIGN)
+                    late_s = keep.tile([P, PASSES * N + M], U8, name="late_s", align_bytes=ALIGN)
+                    first = 0
                     for width, rounded in late_bf:
-                        cols = slice(lo, lo + width)
+                        cols = slice(first, first + width)
                         nc.vector.quantize_mx(out=late_c[:, cols].bitcast(FP8X4), scales=late_s[:, cols], in_=rounded[:])
-                        lo += width
-                now = nxt
+                        first += width
+                now = following
 
         w3_q = [(late_c[:, a * N : (a + 1) * N], late_s[:, a * N : (a + 1) * N]) for a in range(PASSES)]
         z0_c = late_c[:, PASSES * N :]
         z0_s = late_s[:, PASSES * N :]
+
         out_by_tile = out.rearrange("(n p) m -> p n m", p=P)
         with tc.psum_pool(name="stage2", bufs=8) as psum2:
             lo = 0
-            for c, width in enumerate(LAST_CHUNKS):
+            for c, width in enumerate(CHUNKS):
                 hi = lo + width
-                z1 = keep.tile([P, PACK, width], F32, name="z1_%d" % c, tag="tail%d" % (c % 3), align_bytes=64)
+                z1 = keep.tile(
+                    [P, PACK, width], F32, name="z1_%d" % c, tag="chunk%d" % (c % CHUNK_SLOTS), align_bytes=ALIGN
+                )
                 for t in range(PACK):
-                    fetch(z1[:, t, :], 1, t, lo, hi)
-                z1_q = round_and_quantize(z1[:], width, "z1q%d" % lo, keep, "tail%d" % ((c + 2) % 3))
-                moving = ((z0_c[:, lo:hi], z0_s[:, lo:hi]), (z1_q[0][:], z1_q[1][:]))
+                    fetch(z1[:, t, :], PACK + t, lo, hi)
+                z1_bf = round_rows(z1[:], width, "chunk%d" % ((c + 2) % CHUNK_SLOTS))
+                z1_c, z1_s = quantize(width, z1_bf[:], "z1q%d" % c)
+                moving = ((z0_c[:, lo:hi], z0_s[:, lo:hi]), (z1_c[:], z1_s[:]))
                 result = ring.tile([P, N_TILES, width], F32, name="result", tag="result", bufs=3)
                 for n in range(N_TILES):
                     rows = slice(n * P, (n + 1) * P)
@@ -305,7 +314,7 @@ def tile_list_duct_mode_features_kernel(
                             start=False,
                             stop=(a == PASSES - 1),
                         )
-                    y2 = ring.tile([P, width], F32, name="y2", tag="y2", bufs=3)
+                    y2 = ring.tile([P, width], F32, name="y2", tag="y2", bufs=N_TILES)
                     nc.scalar.copy(out=y2[:], in_=acc[:, width:])
                     nc.vector.scalar_tensor_tensor(
                         result[:, n, :], acc[:, :width], bias_sb[:, n : n + 1], y2[:], ALU.add, ALU.max

from contextlib import ExitStack

import concourse.mybir as mybir

K, T, S, H, T2, M, N = 512, 4096, 1024, 1024, 2048, 1024, 384
FLOPS = 2 * (2 * K * H * S + 2 * H * N * M)

F32 = mybir.dt.float32
BF16 = mybir.dt.bfloat16
I32 = mybir.dt.int32
U32 = mybir.dt.uint32
U16 = mybir.dt.uint16
U8 = mybir.dt.uint8
FP8X4 = mybir.dt.float8_e4m3fn_x4
FP4X4 = mybir.dt.float4_e2m1fn_x4
ACT = mybir.ActivationFunctionType
ALU = mybir.AluOpType

P = 128
PACK = 4
K_PASS = P * PACK
GROUP = 16
BANK = 512
ALIGN = 64
PASSES = H // K_PASS
SLICES = PASSES * PACK
N_TILES = N // P
EARLY_PAGES = 2
HALVES = ((0, 512), (512, 1024))
FIRST_PIECES = ((0, 256), (256, 512), (512, 1024))
CHUNKS = (256, 256, 256, 128, 128)
CHUNK_SLOTS = 3


def tile_list_duct_mode_features_kernel(
    tc, tab_words, tab_scales, offs, w1_words, w1_scales, w2, offs2, wgs, offs3, flow, liner, w3, bias,
    w4_words, w4_scales, out,
):
    nc = tc.nc

    with ExitStack() as ctx:
        keep = ctx.enter_context(tc.tile_pool(name="keep", bufs=1))
        ring = ctx.enter_context(tc.tile_pool(name="ring", bufs=2))

        def load_scale_rows(scales, rows):
            by_i = rows.rearrange("a (quadrant i) c -> i quadrant a c", i=4)
            for i in range(4):
                nc.sync.dma_start(out=scales[i:P:32, :, :].bitcast(I32), in_=by_i[i].bitcast(I32))

        idx1 = keep.tile([P, S // GROUP], U16, name="idx1")
        idx2 = keep.tile([P, S // GROUP], U16, name="idx2")
        idx3 = keep.tile([P, M // GROUP], U16, name="idx3")
        w1_raw = keep.tile([P, 2 * H], U8, name="w1_raw", tag="w1_then_vectors")
        w1s_raw = keep.tile([P, H], U8, name="w1s_raw", tag="v_c1", align_bytes=ALIGN)
        table_s = keep.tile([P, T], U8, name="table_s", tag="v_c0", align_bytes=ALIGN)
        nc.gpsimd.memset(w1s_raw[:].bitcast(I32), 0)
        nc.vector.memset(table_s[:].bitcast(I32), 0)
        nc.sync.dma_start(idx1[:], offs)
        nc.sync.dma_start(out=w1_raw[:].bitcast(I32), in_=w1_words[0].bitcast(I32))
        load_scale_rows(w1s_raw[:].rearrange("p (a c) -> p a c", a=1), w1_scales)
        load_scale_rows(table_s[:].rearrange("p (a c) -> p a c", a=1), tab_scales)
        nc.sync.dma_start(idx2[:], offs2)
        nc.sync.dma_start(idx3[:], offs3)
        table = keep.tile([P, T], U32, name="table", tag="weights_raw", align_bytes=ALIGN)
        nc.sync.dma_start(out=table[:].bitcast(I32), in_=tab_words[0].rearrange("p t i -> p (t i)").bitcast(I32))

        w2_by_half = w2.rearrange("(p j) (b c) -> b p j c", j=PACK, b=PASSES)

        def load_w2(b, tag):
            raw = keep.tile([P, PACK, K_PASS], F32, name="w2_raw%d" % b, tag=tag, align_bytes=ALIGN)
            nc.sync.dma_start(out=raw[:], in_=w2_by_half[b])
            return raw

        w2_raw0 = load_w2(0, "w2_then_w4s")

        def new_page(engine, number):
            page = keep.tile([P, T2], F32, name="page%d" % number, tag="page%d" % number, align_bytes=ALIGN)
            engine.memset(page[:], 0.0)
            return page

        pages = [new_page(nc.vector, number) for number in range(EARLY_PAGES)]

        w1_c = keep.tile([P, 2 * H], U8, name="w1_c", align_bytes=ALIGN)
        nc.vector.tensor_copy(
            out=w1_c[:].bitcast(U16).rearrange("p (b t q) -> p b t q", b=PASSES, t=PACK),
            in_=w1_raw[:].bitcast(U16).rearrange("p (b q t) -> p b t q", b=PASSES, t=PACK),
        )
        vectors = keep.tile([P, S + 2 * SLICES], F32, name="vectors", tag="w1_then_vectors")
        wgs_sb = vectors[:, 0:S]
        nc.sync.dma_start(out=wgs_sb, in_=wgs)
        w1_s = keep.tile([P, H], U8, name="w1_s", align_bytes=ALIGN)
        nc.vector.tensor_copy(
            out=w1_s[:].rearrange("p (b t q) -> p b t q", b=PASSES, t=PACK),
            in_=w1s_raw[:].rearrange("p (b q t) -> p b t q", b=PASSES, t=PACK),
        )

        liner_sb = vectors[:, S : S + SLICES]
        bias_sb = vectors[:, S + SLICES : S + SLICES + N_TILES]
        nc.sync.dma_start(
            out=liner_sb.rearrange("p (b t) -> p b t", b=PASSES),
            in_=liner.rearrange("(b p t) -> p b t", b=PASSES, t=PACK),
        )
        with nc.allow_non_contiguous_dma(reason="one bias value for each partition and output tile"):
            nc.sync.dma_start(out=bias_sb, in_=bias.rearrange("(n p) -> p n", p=P))

        flow_by_pass = flow.rearrange("(b p t) m -> b p t m", b=PASSES, t=PACK)
        flows = []

        def add_liner(s):
            nc.scalar.activation(flows[s], flows[s], ACT.Identity, bias=liner_sb[:, s : s + 1])

        def quantize(width, rounded, name):
            codes = keep.tile([P, width], U32, name=name + "_c", align_bytes=ALIGN)
            scales = keep.tile([P, width], U8, name=name + "_s", align_bytes=ALIGN)
            nc.vector.quantize_mx(out=codes[:].bitcast(FP8X4), scales=scales[:], in_=rounded)
            return codes, scales

        def quantize_w2(copy, raw, b, t0, t1, tag):
            count = t1 - t0
            rounded = keep.tile([P, count * K_PASS], BF16, name="w2_bf%d_%d" % (b, t0), tag=tag, align_bytes=ALIGN)
            copy(
                out=rounded[:].rearrange("p (t q j) -> p q j t", t=count, j=PACK),
                in_=raw[:].rearrange("p j (q t) -> p q j t", t=PACK)[:, :, :, t0:t1],
            )
            codes, scales = quantize(count * P, rounded[:], "w2q%d_%d" % (b, t0))
            return [(codes[:, i * P : (i + 1) * P], scales[:, i * P : (i + 1) * P]) for i in range(count)]

        def round_rows(rows, width, tag):
            rounded = keep.tile([P, PACK * width], BF16, name="rounded", tag=tag, align_bytes=ALIGN)
            nc.scalar.copy(
                out=rounded[:].rearrange("p (c i t) -> p c t i", i=4, t=PACK),
                in_=rows.rearrange("p t (c i) -> p c t i", i=4),
            )
            return rounded

        v_s = keep.tile([P, S], U8, name="v_s", align_bytes=ALIGN)
        nc.vector.tensor_copy(v_s[:], table_s[:].indirect(idx1[:]))
        v_c = []
        for half, (lo, hi) in enumerate(HALVES):
            words = keep.tile([P, hi - lo], U32, name="v_c%d" % half, tag="v_c%d" % half, align_bytes=ALIGN)
            nc.vector.tensor_copy(words[:], table[:].indirect(idx1[:, lo // GROUP : hi // GROUP]))
            v_c.append(words)

        w2_q = quantize_w2(nc.vector.tensor_copy, w2_raw0, 0, 0, 1, "flow0")
        w2_raw1 = load_w2(1, "weights_raw")

        def load_flow_slice(s):
            rows = keep.tile([P, M], F32, name="flow%d" % s, tag="flow%d" % s, align_bytes=ALIGN)
            nc.sync.dma_start(out=rows[:], in_=flow_by_pass[0, :, s, :])
            flows.append(rows[:])

        load_flow_slice(0)
        z0 = keep.tile([P, PACK, M], F32, name="z0")

        def page_of(s):
            return pages[s % EARLY_PAGES if s < PACK else s - PACK]

        def fetch(dst, s, lo, hi):
            picked = page_of(s)[:].indirect(idx3[:, lo // GROUP : hi // GROUP])
            nc.vector.tensor_tensor(dst, picked, flows[s][:, lo:hi], ALU.add)

        with tc.psum_pool(name="stage1", bufs=2) as psum1:

            def features(s, pieces):
                if s == 0:
                    phase = keep.tile([P, S], F32, name="phase0", tag="flow3", align_bytes=ALIGN)
                    level = keep.tile([P, S], F32, name="level0", tag="flow2", align_bytes=ALIGN)
                else:
                    phase = ring.tile([P, S], F32, name="phase", tag="phase")
                    if EARLY_PAGES <= s < PACK:
                        level = keep.tile([P, S], F32, name="level%d" % s, tag="page%d" % s, align_bytes=ALIGN)
                    else:
                        level = ring.tile([P, S], F32, name="level", tag="level")
                for lo, hi in pieces:
                    cols = slice(lo, hi)
                    words = v_c[lo // BANK][:, lo % BANK : lo % BANK + hi - lo]
                    acc1 = psum1.tile([P, hi - lo], F32, name="acc1", tag="acc1")
                    nc.tensor.matmul_mx(
                        out=acc1[:],
                        lhsT=w1_c[:, s * 2 * P : (s + 1) * 2 * P].bitcast(FP4X4),
                        lhsT_scale=w1_s[:, s * P : (s + 1) * P],
                        rhs=words.bitcast(FP8X4),
                        rhs_scale=v_s[:, cols],
                        start=True,
                        stop=True,
                    )
                    nc.scalar.activation(phase[:, cols], acc1[:], ACT.Tanh)
                    acc2 = psum1.tile([P, hi - lo], F32, name="acc2", tag="acc2")
                    nc.tensor.matmul_mx(
                        out=acc2[:],
                        lhsT=w2_q[s][0].bitcast(FP8X4),
                        lhsT_scale=w2_q[s][1],
                        rhs=words.bitcast(FP8X4),
                        rhs_scale=v_s[:, cols],
                        start=True,
                        stop=True,
                    )
                    nc.scalar.activation(level[:, cols], acc2[:], ACT.Abs)
                return phase, level

            def product(engine, weighted, pair, lo, hi):
                phase, level = pair
                engine.tensor_tensor(weighted[:, lo:hi], level[:, lo:hi], wgs_sb[:, lo:hi], ALU.mult)
                engine.tensor_tensor(weighted[:, lo:hi], weighted[:, lo:hi], phase[:, lo:hi], ALU.mult)

            def put(weighted, s, lo, hi):
                places = page_of(s)[:].indirect(idx2[:, lo // GROUP : hi // GROUP])
                nc.vector.tensor_copy(places, weighted[:, lo:hi])

            def new_weighted(s):
                if s == 1:
                    return keep.tile([P, S], F32, name="weighted1", tag="flow3", align_bytes=ALIGN)
                if 2 <= s < 2 + PACK:
                    return keep.tile([P, S], F32, name="weighted%d" % s, tag="flow%d" % (s - 2), align_bytes=ALIGN)
                return ring.tile([P, S], F32, name="weighted", tag="weighted", align_bytes=ALIGN)

            pair = features(0, FIRST_PIECES)
            w2_q.extend(quantize_w2(nc.scalar.copy, w2_raw0, 0, 1, PACK, "flow1"))
            load_flow_slice(1)
            now = new_weighted(0)
            for lo, hi in FIRST_PIECES:
                product(nc.vector, now, pair, lo, hi)
                if lo == 0:
                    put(now, 0, lo, hi)
            put(now, 0, FIRST_PIECES[0][1], S)
            load_flow_slice(2)

            for s in range(SLICES):
                following = None
                if s + 1 < SLICES:
                    following = new_weighted(s + 1)
                    product(nc.gpsimd, following, features(s + 1, HALVES), 0, S)
                    if EARLY_PAGES <= s + 1 < PACK:
                        pages.append(new_page(nc.gpsimd, s + 1))
                if s > 0:
                    put(now, s, 0, S)
                if s < PACK:
                    add_liner(s)
                    fetch(z0[:, s, :], s, 0, M)
                if s == 1:
                    load_flow_slice(3)
                    w2_q.extend(quantize_w2(nc.scalar.copy, w2_raw1, 1, 0, PACK, "w2bf_then_flow"))
                    flow_late = keep.tile([P, PACK, M], F32, name="flow_late", tag="w2bf_then_flow", align_bytes=ALIGN)
                    nc.sync.dma_start(out=flow_late[:], in_=flow_by_pass[1])
                    flows.extend(flow_late[:, t, :] for t in range(PACK))
                    w4_s = keep.tile([P, PASSES, N], U8, name="w4_s", tag="w2_then_w4s", align_bytes=ALIGN)
                    nc.vector.memset(w4_s[:].rearrange("p a c -> p (a c)").bitcast(I32), 0)
                    load_scale_rows(w4_s[:], w4_scales)
                    w3_raw = keep.tile([P, PASSES, PACK, N], F32, name="w3_raw", tag="weights_raw", align_bytes=ALIGN)
                    nc.sync.dma_start(
                        out=w3_raw[:].rearrange("p a j n -> p a (j n)"),
                        in_=w3.rearrange("(a p j) n -> p a (j n)", a=PASSES, j=PACK),
                    )
                if s == SLICES - 2:
                    late_bf = []
                    for a in range(PASSES):
                        late_bf.append((N, round_rows(w3_raw[:, a], N, "w3_bf%d" % a)))
                    w4_c = keep.tile([P, PASSES, N], U32, name="w4_c", tag="weights_raw", align_bytes=ALIGN)
                    nc.sync.dma_start(
                        out=w4_c[:].bitcast(I32),
                        in_=w4_words.rearrange("a p n i -> p a (n i)").bitcast(I32),
                    )
                    for t in range(PACK):
                        add_liner(PACK + t)
                    for half, (lo, hi) in enumerate(HALVES):
                        late_bf.append((hi - lo, round_rows(z0[:, :, lo:hi], hi - lo, "v_c%d" % half)))
                    late_c = ring.tile([P, PASSES * N + M], U32, name="late_c", tag="weighted", align_bytes=ALIGN)
                    late_s = keep.tile([P, PASSES * N + M], U8, name="late_s", align_bytes=ALIGN)
                    first = 0
                    for width, rounded in late_bf:
                        cols = slice(first, first + width)
                        nc.vector.quantize_mx(out=late_c[:, cols].bitcast(FP8X4), scales=late_s[:, cols], in_=rounded[:])
                        first += width
                now = following

        w3_q = [(late_c[:, a * N : (a + 1) * N], late_s[:, a * N : (a + 1) * N]) for a in range(PASSES)]
        z0_c = late_c[:, PASSES * N :]
        z0_s = late_s[:, PASSES * N :]

        out_by_tile = out.rearrange("(n p) m -> p n m", p=P)
        with tc.psum_pool(name="stage2", bufs=8) as psum2:
            lo = 0
            for c, width in enumerate(CHUNKS):
                hi = lo + width
                z1 = keep.tile(
                    [P, PACK, width], F32, name="z1_%d" % c, tag="chunk%d" % (c % CHUNK_SLOTS), align_bytes=ALIGN
                )
                for t in range(PACK):
                    fetch(z1[:, t, :], PACK + t, lo, hi)
                z1_bf = round_rows(z1[:], width, "chunk%d" % ((c + 2) % CHUNK_SLOTS))
                z1_c, z1_s = quantize(width, z1_bf[:], "z1q%d" % c)
                moving = ((z0_c[:, lo:hi], z0_s[:, lo:hi]), (z1_c[:], z1_s[:]))
                result = ring.tile([P, N_TILES, width], F32, name="result", tag="result", bufs=3)
                for n in range(N_TILES):
                    rows = slice(n * P, (n + 1) * P)
                    acc = psum2.tile([P, 2 * width], F32, name="acc", tag="acc")
                    for a in range(PASSES):
                        codes, scales = moving[a]
                        nc.tensor.matmul_mx(
                            out=acc[:, :width],
                            lhsT=w3_q[a][0][:, rows].bitcast(FP8X4),
                            lhsT_scale=w3_q[a][1][:, rows],
                            rhs=codes.bitcast(FP8X4),
                            rhs_scale=scales,
                            start=(a == 0),
                            stop=False,
                        )
                        nc.tensor.matmul_mx(
                            out=acc[:, width:],
                            lhsT=w4_c[:, a, rows].bitcast(FP8X4),
                            lhsT_scale=w4_s[:, a, rows],
                            rhs=codes.bitcast(FP8X4),
                            rhs_scale=scales,
                            start=False,
                            stop=(a == PASSES - 1),
                        )
                    y2 = ring.tile([P, width], F32, name="y2", tag="y2", bufs=N_TILES)
                    nc.scalar.copy(out=y2[:], in_=acc[:, width:])
                    nc.vector.scalar_tensor_tensor(
                        result[:, n, :], acc[:, :width], bias_sb[:, n : n + 1], y2[:], ALU.add, ALU.max
                    )
                nc.sync.dma_start(out=out_by_tile[:, :, lo:hi], in_=result[:])
                lo = hi
